import numpy as np
import ml_dtypes


def mxq(x, axis, fmt="e4m3"):
    dtype, down = {"e4m3": (ml_dtypes.float8_e4m3fn, 7), "e5m2": (ml_dtypes.float8_e5m2, 14)}[fmt]
    v = np.moveaxis(np.asarray(x, np.float32).astype(ml_dtypes.bfloat16).astype(np.float64), axis, -1)
    blocks = v.reshape(v.shape[:-1] + (-1, 32))
    amax = np.abs(blocks).max(-1, keepdims=True)
    byte = np.maximum(np.where(amax > 0, np.frexp(amax)[1] - 1 + 127, 0) - down, 1)
    scale = np.exp2(byte - 127.0)
    codes = (blocks / scale).astype(np.float32).astype(dtype).astype(np.float64)
    return np.moveaxis((codes * scale).reshape(v.shape), -1, axis)


WIDE = False


def mx_kscale(k):
    if not WIDE:
        return np.ones(k)
    levels = np.array([10, -10, 5, -5, 0])
    if k % 512:
        return np.exp2(np.random.permutation(np.resize(levels, k // 32))).repeat(32)
    a = np.empty((k // 512, 16))
    for p in range(k // 512):
        a[p, :8] = np.random.permutation(np.resize(levels, 8))
        for g in range(8):
            far = levels[np.abs(levels - a[p, g]) >= 10]
            a[p, g + 8] = far[np.random.randint(len(far))]
    return np.exp2(a.ravel()).repeat(32)


def f64(x):
    return np.asarray(x).astype(np.float64)


def striped(idx):
    return np.tile(idx.reshape(-1, 16).T, (8, 1)).astype(np.uint16)


def unstriped(offs):
    return offs[:16].T.reshape(-1).astype(np.int64)


E2M1 = np.array([0.0, 0.5, 1.0, 1.5, 2.0, 3.0, 4.0, 6.0, -0.0, -0.5, -1.0, -1.5, -2.0, -3.0, -4.0, -6.0])


def pack_weight(w, fmt):
    k, n = w.shape
    w = f64(np.asarray(w, np.float32).astype(ml_dtypes.bfloat16)).reshape(k // 32, 32, n)
    amax = np.abs(w).max(1)
    if fmt == "e4m3":
        byte = np.frexp(amax)[1] - 1 + 127 - 7
    else:
        mant, ex = np.frexp(amax / 6.0)
        byte = np.where(mant > 0.5, ex, ex - 1) + 127
    byte = np.clip(np.where(amax > 0, byte, 1), 1, 254)
    scaled = (w * np.exp2(127.0 - byte)[:, None, :]).reshape(k, n).astype(np.float32)
    by_word = np.ascontiguousarray(scaled.reshape(k // 512, 128, 4, n).transpose(0, 1, 3, 2))
    if fmt == "e4m3":
        words = by_word.astype(ml_dtypes.float8_e4m3fn).view(np.uint8)
    else:
        c = by_word.astype(ml_dtypes.float4_e2m1fn).view(np.uint8) & 0xF
        words = (c[..., 0::2] | (c[..., 1::2] << 4)).reshape(k // 512, 128, 2 * n)
    return np.ascontiguousarray(words), np.ascontiguousarray(byte.astype(np.uint8).reshape(k // 512, 16, n))


def unpack_weight(words, scales, fmt):
    g, _, n = scales.shape
    words = np.ascontiguousarray(words).reshape(g, 128, n, -1)
    if fmt == "e4m3":
        vals = words.view(ml_dtypes.float8_e4m3fn).astype(np.float64)
    else:
        nib = np.empty((g, 128, n, 4), np.uint8)
        nib[..., 0::2] = words & 0xF
        nib[..., 1::2] = words >> 4
        vals = E2M1[nib]
    vals = vals * np.repeat(np.exp2(scales.astype(np.float64) - 127.0), 8, axis=1)[..., None]
    return vals.transpose(0, 1, 3, 2).reshape(g * 512, n)


def gelu(v):
    return 0.5 * v * (1.0 + np.tanh(np.sqrt(2.0 / np.pi) * (v + 0.044715 * v**3)))


def bf(x):
    return np.asarray(x, np.float32).astype(ml_dtypes.bfloat16)


def planes(Y):
    n, m = Y.shape
    b = f64(bf(Y)).reshape(n // 32, 32, m)
    amax = np.abs(b).max(1)
    byte = np.clip(np.where(amax > 0, np.frexp(amax)[1] - 1 + 127 - 7, 1), 1, 254)
    codes = (b * np.exp2(127.0 - byte)[:, None, :]).reshape(n, m).astype(np.float32).astype(ml_dtypes.float8_e4m3fn).view(np.uint8)
    words = codes.reshape(n // 512, 128, 4, m).transpose(0, 1, 3, 2)
    return np.ascontiguousarray(words), np.ascontiguousarray(byte.astype(np.uint8).reshape(n // 512, 16, m))


K, K2, H, N, T, T3, S, T2 = 1024, 512, 1024, 512, 2048, 1024, 512, 1024

def setup_inputs():
    n = np.random.standard_normal
    s, s2, u = mx_kscale(K)[:, None], mx_kscale(K2)[:, None], mx_kscale(H)[:, None]
    tab_words, tab_scales = pack_weight(n((K, T)) * s, "e4m3")
    tab2_words, tab2_scales = pack_weight(n((K2, T3)) * s2, "e4m3")
    w1_words, w1_scales = pack_weight(1.3 * n((K, H)) / np.sqrt(K) / s, "e2m1")
    w4_words, w4_scales = pack_weight(0.4 * n((H, N)) / np.sqrt(H) / u * np.exp(0.8 * n(N)), "e4m3")
    return {
        "tab_words": tab_words, "tab_scales": tab_scales,
        "tab2_words": tab2_words, "tab2_scales": tab2_scales,
        "offs": striped(np.random.permutation(T)[:S]), "offs2": striped(np.random.permutation(T3)[:S]),
        "offs3": striped(np.random.permutation(T2)[:S]), "offs4": striped(np.random.permutation(T2)[:S]),
        "w1_words": w1_words, "w1_scales": w1_scales,
        "w2": (1.6 * n((K2, H)) / np.sqrt(K2) / s2).astype(np.float32),
        "w3": (1.1 * n((H, N)) / np.sqrt(H) / u).astype(np.float32),
        "w4_words": w4_words, "w4_scales": w4_scales,
        "forecast": (0.8 * n((H, T2))).astype(np.float32),
        "gain": (np.exp(0.3 * n(H)) * u[:, 0]).astype(np.float32),
        "wg1": np.exp(0.3 * n((128, S))).astype(np.float32),
        "wg2": np.exp(0.3 * n((128, S))).astype(np.float32),
    }

def reference(tab_words, tab_scales, tab2_words, tab2_scales, offs, offs2, offs3, offs4, w1_words, w1_scales, w2, w3, w4_words, w4_scales, forecast, gain, wg1, wg2):
    v = unpack_weight(tab_words, tab_scales, "e4m3")[:, unstriped(offs)]
    v2 = unpack_weight(tab2_words, tab2_scales, "e4m3")[:, unstriped(offs2)]
    h1 = np.tanh(unpack_weight(w1_words, w1_scales, "e2m1").T @ v)
    b = mxq(f64(w2), 0, "e4m3").T @ v2
    h2 = b / (1.0 + np.exp(-b))
    pa = np.zeros((H, T2))
    pa[:, unstriped(offs3)] = np.tile(f64(wg1), (H // 128, 1)) * h1
    pb = np.zeros((H, T2))
    pb[:, unstriped(offs4)] = np.tile(f64(wg2), (H // 128, 1)) * h2
    z = f64(gain)[:, None] * (np.maximum(pa, f64(forecast)) + pb)
    zq = mxq(z, 0, "e4m3")
    bent = np.tanh(mxq(f64(w3), 0, "e4m3").T @ zq)
    y = bent + (unpack_weight(w4_words, w4_scales, "e4m3").T @ zq)
    words, scales = planes(y)
    return y, words, scales

@@ -1,0 +1,483 @@
+from contextlib import ExitStack
+
+import concourse.mybir as mybir
+from concourse.masks import make_identity
+
+K, K2, H, N, T, T3, S, T2 = 1024, 512, 1024, 512, 2048, 1024, 512, 1024
+FLOPS = 2 * S * H * (K + K2) + 2 * 2 * H * N * T2
+
+F32 = mybir.dt.float32
+BF16 = mybir.dt.bfloat16
+I32 = mybir.dt.int32
+U32 = mybir.dt.uint32
+U16 = mybir.dt.uint16
+U8 = mybir.dt.uint8
+FP8X4 = mybir.dt.float8_e4m3fn_x4
+FP4X4 = mybir.dt.float4_e2m1fn_x4
+ACT = mybir.ActivationFunctionType
+ALU = mybir.AluOpType
+
+P = 128
+PACK = 4
+KP = P * PACK
+SLICES = H // P
+BLOCKS = T2 // P
+CHUNKS = [(0, 256), (256, 256), (512, 256), (768, 128), (896, 128)]
+
+
+def tile_list_sounder_bias_features_kernel(
+    tc, tab_words, tab_scales, tab2_words, tab2_scales, offs, offs2, offs3, offs4,
+    w1_words, w1_scales, w2, w3, w4_words, w4_scales, forecast, gain, wg1, wg2,
+    out_0, out_1, out_2,
+):
+    nc = tc.nc
+    with ExitStack() as ctx:
+        keep = ctx.enter_context(tc.tile_pool(name="keep", bufs=1))
+        late = ctx.enter_context(tc.tile_pool(name="late", bufs=1))
+        tables = ctx.enter_context(tc.tile_pool(name="tables", bufs=1))
+        work = ctx.enter_context(tc.tile_pool(name="work", bufs=2))
+        psum = ctx.enter_context(tc.psum_pool(name="psum", bufs=2))
+
+        def held(name, shape, dtype):
+            return keep.tile(shape, dtype, name=name, align_bytes=64)
+
+        def laid(name, shape, dtype, offset):
+            return late.tile(shape, dtype, name=name, align_bytes=64, offset=offset)
+
+        def stage_tile(shape):
+            return work.tile(shape, BF16, name="stage", tag="stage", bufs=6, align_bytes=64)
+
+        def row_tile(i, shape):
+            place = i % 5
+            return tables.tile(shape, F32, name="rows%d" % place, align_bytes=64, offset=4096 * place)
+
+        def feature_tile():
+            return work.tile([P, S], F32, name="feature", tag="feature", bufs=5, align_bytes=64)
+
+        def raw_tile(shape, dtype):
+            return work.tile(shape, dtype, name="raw", tag="raw", bufs=2, align_bytes=64)
+
+        def bank(tag, bufs, shape):
+            return psum.tile(shape, F32, name=tag, tag=tag, bufs=bufs)
+
+        def zero_bytes(engine, tile):
+            engine.memset(tile[:].bitcast(I32), 0)
+
+        def load_words(tile_ap, words):
+            nc.sync.dma_start(out=tile_ap.bitcast(I32), in_=words.rearrange("p c i -> p (c i)").bitcast(I32))
+
+        def load_planes(tile, scales):
+            passes = scales.shape[0]
+            for q in range(4):
+                nc.sync.dma_start(
+                    out=tile[32 * q : 32 * q + 4, :].bitcast(I32).rearrange("r (a w) -> r a w", a=passes),
+                    in_=scales[:, 4 * q : 4 * q + 4, :].bitcast(I32).rearrange("a r w -> r a w"),
+                )
+
+        lists = [held("list%d" % i, [P, S // 16], U16) for i in range(4)]
+        tab2_w = tables.tile([P, T3], U32, name="tab2_w", align_bytes=64, offset=0)
+        tab_w = [
+            tables.tile([P, T], U32, name="tab_w%d" % a, align_bytes=64, offset=4096 + 8192 * a) for a in range(2)
+        ]
+        tab_s = tables.tile([P, 2 * T], U8, name="tab_s", align_bytes=64, offset=20480)
+        w4_raw_s = tables.tile([P, N], U8, name="w4_raw_s", align_bytes=64, offset=20480)
+        tab2_s = held("tab2_s", [P, T3], U8)
+        v_w = [held("v_w%d" % a, [P, S], U32) for a in range(2)]
+        v2_w = held("v2_w", [P, S], U32)
+        v2_s = held("v2_s", [P, S], U8)
+        w1_w = held("w1_w", [P, 2, 2 * H], U8)
+        w1_s = held("w1_s", [P, 2 * H], U8)
+        wg2_neg = laid("wg2_neg", [P, S], F32, 0)
+        last_h_b = laid("last_h_b", [P, S], F32, 2048)
+        w3_s = [laid("w3_s%d" % a, [P, N], U8, 512 * a) for a in range(2)]
+        w4_s = laid("w4_s", [P, N], U8, 1024)
+        z0_s = [laid("z0_s0", [P, 512], U8, 1536), laid("z0_s1", [P, 512], U8, 2048)]
+        w4_w = laid("w4_w", [P, 2, N], U32, 2560)
+        first_h_b = laid("first_h_b", [P, S], F32, 6656)
+        v_s = [laid("v_s%d" % a, [P, S], U8, 6656 + 512 * a) for a in range(2)]
+        second_h_b = tables.tile([P, S], F32, name="second_h_b", align_bytes=64, offset=19456)
+        own_h_b = {0: first_h_b, 1: second_h_b, SLICES - 1: last_h_b}
+        w3_w = [held("w3_w%d" % a, [P, N], U32) for a in range(2)]
+        wg1_t = held("wg1_t", [P, S], F32)
+        wg2_t = held("wg2_t", [P, S], F32)
+        gain_t = held("gain_t", [P, 2, PACK], F32)
+        ident = held("ident", [P, P], F32)
+        pages_a = [held("page_a%d" % i, [P, T2], F32) for i in range(2)]
+        pages_b = [held("page_b%d" % i, [P, T2], F32) for i in range(3)]
+        w2_pieces = [(0, 1), (1, 1), (2, 2), (4, 2), (6, 2)]
+        w2_w = [held("w2_w%d" % i, [P, P * n], U32) for i, (s0, n) in enumerate(w2_pieces)]
+        w2_s = [held("w2_s%d" % i, [P, P * n], U8) for i, (s0, n) in enumerate(w2_pieces)]
+        z0_w = [held("z0_w%d" % h, [P, 512], U32) for h in range(2)]
+        z1_w = [held("z1_w%d" % c, [P, width], U32) for c, (m0, width) in enumerate(CHUNKS)]
+        z1_s = [held("z1_s%d" % c, [P, width], U8) for c, (m0, width) in enumerate(CHUNKS)]
+        y_w = [held("y_w%d" % c, [P, width], U32) for c, (m0, width) in enumerate(CHUNKS)]
+        y_s = held("y_s", [P, T2], U8)
+        excess = [[held("excess%d%d" % (g, h), [P, 4, PACK, P], F32) for h in range(2)] for g in range(2)]
+        placed = [[held("placed%d%d" % (g, h), [P, 4, PACK, P], F32) for h in range(2)] for g in range(2)]
+
+        zero_bytes(nc.gpsimd, tab2_s)
+        for plane in (tab_s, w1_s):
+            zero_bytes(nc.vector, plane)
+        nc.vector.memset(pages_b[0][:], 0.0)
+        for page in (pages_b[1], pages_a[0], pages_a[1], pages_b[2]):
+            nc.gpsimd.memset(page[:], 0.0)
+        make_identity(nc, ident[:])
+
+        z1_acc, w4_raw, y_banks = {}, {}, []
+        w2_raw, w3_raw, w2_stage, w3_stage, f_rows = {}, {}, {}, {}, {}
+        h_a, h_b, z0_rows, z0_stage, z1_stage, y_rows, y_stage = {}, {}, {}, {}, {}, {}, {}
+
+        def load_w2(i):
+            s0, n = w2_pieces[i]
+            w2_raw[i] = raw_tile([P, PACK, P * n], F32)
+            nc.sync.dma_start(out=w2_raw[i][:], in_=w2[:, P * s0 : P * (s0 + n)].rearrange("(p j) c -> p j c", j=PACK))
+
+        def cast_w2(i):
+            n = w2_pieces[i][1]
+            w2_stage[i] = stage_tile([P, P * n * PACK])
+            nc.scalar.copy(
+                out=w2_stage[i][:].rearrange("p (c i j) -> p c j i", i=4, j=PACK),
+                in_=w2_raw[i][:].rearrange("p j (c i) -> p c j i", i=4),
+            )
+
+        def quantize_w2(i):
+            nc.vector.quantize_mx(out=w2_w[i][:].bitcast(FP8X4), scales=w2_s[i][:], in_=w2_stage[i][:])
+
+        def load_w3(i):
+            a, half = divmod(i, 2)
+            w3_raw[i] = raw_tile([P, PACK, 256], F32)
+            nc.sync.dma_start(
+                out=w3_raw[i][:],
+                in_=w3[KP * a : KP * (a + 1), 256 * half : 256 * (half + 1)].rearrange("(p j) c -> p j c", j=PACK),
+            )
+
+        def cast_w3(i):
+            a, half = divmod(i, 2)
+            if half == 0:
+                w3_stage[a] = stage_tile([P, PACK, P, PACK])
+            nc.scalar.copy(
+                out=w3_stage[a][:, :, 64 * half : 64 * (half + 1), :].rearrange("p t q j -> p q j t"),
+                in_=w3_raw[i][:].rearrange("p j (q t) -> p q j t", t=PACK),
+            )
+
+        def quantize_w3(a):
+            nc.vector.quantize_mx(
+                out=w3_w[a][:].bitcast(FP8X4), scales=w3_s[a][:], in_=w3_stage[a][:].rearrange("p t q j -> p (t q j)")
+            )
+
+        def load_w4():
+            w4_raw["words"] = raw_tile([P, 2, N], U32)
+            nc.sync.dma_start(
+                out=w4_raw["words"][:].bitcast(I32), in_=w4_words.rearrange("a p c i -> p a (c i)").bitcast(I32)
+            )
+            zero_bytes(nc.gpsimd, w4_raw_s)
+            for q in range(4):
+                nc.sync.dma_start(
+                    out=w4_raw_s[32 * q : 32 * q + 8, :].bitcast(I32),
+                    in_=w4_scales[:, 4 * q : 4 * q + 4, :].bitcast(I32),
+                )
+
+        def deal_w4():
+            nc.vector.tensor_copy(
+                out=w4_w[:].bitcast(I32).rearrange("p a (t c i) -> p a c t i", t=PACK, i=4),
+                in_=w4_raw["words"][:].bitcast(I32).rearrange("p a (c i t) -> p a c t i", t=PACK, i=4),
+            )
+            nc.vector.tensor_copy(
+                out=w4_s[:].rearrange("p (t q) -> p q t", t=PACK),
+                in_=w4_raw_s[:].rearrange("p (q t) -> p q t", t=PACK),
+            )
+
+        def load_forecast(s):
+            f_rows[s] = row_tile(s, [P, T2])
+            nc.sync.dma_start(out=f_rows[s][:], in_=forecast[P * s : P * (s + 1), :])
+
+        def features_a(s):
+            acc = bank("first", 2, [P, S])
+            for a in range(2):
+                nc.tensor.matmul_mx(
+                    out=acc[:],
+                    lhsT=w1_w[:, a, 2 * P * s : 2 * P * (s + 1)].bitcast(FP4X4),
+                    lhsT_scale=w1_s[:, H * a + P * s : H * a + P * (s + 1)],
+                    rhs=v_w[a][:].bitcast(FP8X4),
+                    rhs_scale=v_s[a][:],
+                    start=(a == 0),
+                    stop=(a == 1),
+                )
+            h_a[s] = feature_tile()
+            nc.scalar.activation(out=h_a[s][:], in_=acc[:], func=ACT.Tanh, scale=-1.0)
+
+        def features_b(s):
+            i = max(j for j, (s0, n) in enumerate(w2_pieces) if s0 <= s)
+            cols = slice(P * (s - w2_pieces[i][0]), P * (s - w2_pieces[i][0] + 1))
+            acc = bank("first", 2, [P, S])
+            nc.tensor.matmul_mx(
+                out=acc[:],
+                lhsT=w2_w[i][:, cols].bitcast(FP8X4),
+                lhsT_scale=w2_s[i][:, cols],
+                rhs=v2_w[:].bitcast(FP8X4),
+                rhs_scale=v2_s[:],
+                start=True,
+                stop=True,
+            )
+            h_b[s] = own_h_b[s] if s in own_h_b else feature_tile()
+            nc.scalar.activation(out=h_b[s][:], in_=acc[:], func=ACT.Silu)
+
+        def place_a(s):
+            nc.vector.tensor_tensor(pages_a[s % 2][:].indirect(lists[2][:]), h_a[s][:], wg1_t[:], ALU.mult)
+
+        def place_b(s):
+            nc.vector.tensor_tensor(pages_b[s % 3][:].indirect(lists[3][:]), h_b[s][:], wg2_neg[:], ALU.mult)
+
+        def add_turned(out, first, second):
+            nc.tensor.matmul(out, lhsT=first, rhs=ident[:], start=True, stop=False, is_transpose=True)
+            nc.tensor.matmul(out, lhsT=second, rhs=ident[:], start=False, stop=True, is_transpose=True)
+
+        def turn_sum(s, first, second, dest, func, scale, blocks):
+            g, quarter = divmod(s, 4)
+            for b0 in range(0, BLOCKS, blocks):
+                acc = bank("turned", 3, [P, blocks, P])
+                for b in range(blocks):
+                    cols = slice(P * (b0 + b), P * (b0 + b + 1))
+                    add_turned(acc[:, b, :], first[:, cols], second[:, cols])
+                half, b1 = divmod(b0, 4)
+                nc.scalar.activation(
+                    out=dest[g][half][:, b1 : b1 + blocks, :, 32 * quarter : 32 * (quarter + 1)],
+                    in_=acc[:].rearrange("m b (p t) -> m b t p", t=PACK),
+                    func=func,
+                    scale=scale,
+                )
+
+        def turn_excess(s):
+            turn_sum(s, f_rows[s], pages_a[s % 2], excess, ACT.Relu, 1.0, 4)
+
+        def turn_placed(s):
+            turn_sum(s, pages_a[s % 2], pages_b[s % 3], placed, ACT.Copy, -1.0, 2 if s == SLICES - 1 else 4)
+
+        def z0_part(half, t):
+            if t == 0:
+                z0_rows[half] = stage_tile([P, PACK, 512])
+            acc = bank("back", 3, [P, 4, P])
+            for b in range(4):
+                add_turned(acc[:, b, :], excess[0][half][:, b, t, :], placed[0][half][:, b, t, :])
+            nc.scalar.activation(
+                out=z0_rows[half][:, t, :],
+                in_=acc[:].rearrange("p b m -> p (b m)"),
+                func=ACT.Copy,
+                scale=gain_t[:, 0, t : t + 1],
+            )
+
+        def z0_weave(half, part):
+            if part == 0:
+                z0_stage[half] = stage_tile([P, 512 * PACK])
+            nc.scalar.copy(
+                out=z0_stage[half][:, 1024 * part : 1024 * (part + 1)].rearrange("p (c i t) -> p c t i", i=4, t=PACK),
+                in_=z0_rows[half][:, :, 256 * part : 256 * (part + 1)].rearrange("p t (c i) -> p c t i", i=4),
+            )
+
+        def quantize_z0(half):
+            nc.vector.quantize_mx(out=z0_w[half][:].bitcast(FP8X4), scales=z0_s[half][:], in_=z0_stage[half][:])
+
+        def turn_back(acc, source, block, opens):
+            half, b = divmod(block, 4)
+            for t in range(PACK):
+                nc.tensor.matmul(
+                    acc[:, t, :],
+                    lhsT=source[1][half][:, b, t, :],
+                    rhs=ident[:],
+                    start=(opens and t == 0),
+                    stop=(not opens and t == PACK - 1),
+                    is_transpose=True,
+                )
+
+        def open_z1(block):
+            z1_acc[block] = bank("first", 2, [P, PACK, P]) if block in (3, 4) else bank("back", 3, [P, PACK, P])
+            turn_back(z1_acc[block], excess, block, True)
+
+        def make_z1(c):
+            m0, width = CHUNKS[c]
+            z1_stage[c] = stage_tile([P, width // P, P, PACK])
+            for j in range(width // P):
+                block = m0 // P + j
+                if block not in z1_acc:
+                    open_z1(block)
+                acc = z1_acc[block]
+                turn_back(acc, placed, block, False)
+                nc.vector.tensor_tensor(
+                    z1_stage[c][:, j, :, :],
+                    acc[:].rearrange("p t m -> p m t"),
+                    gain_t[:, 1, :].unsqueeze(1).to_broadcast([P, P, PACK]),
+                    ALU.mult,
+                )
+
+        def quantize_z1(c):
+            nc.vector.quantize_mx(
+                out=z1_w[c][:].bitcast(FP8X4), scales=z1_s[c][:], in_=z1_stage[c][:].rearrange("p j m t -> p (j m t)")
+            )
+
+        def second_product(acc, c, t, weight_words, weight_scales):
+            m0, width = CHUNKS[c]
+            half, first = divmod(m0, 512)
+            cols = slice(first, first + width)
+            moving = [(z0_w[half][:, cols], z0_s[half][:, cols]), (z1_w[c][:], z1_s[c][:])]
+            for a in range(2):
+                nc.tensor.matmul_mx(
+                    out=acc,
+                    lhsT=weight_words(a)[:, P * t : P * (t + 1)].bitcast(FP8X4),
+                    lhsT_scale=weight_scales(a)[:, P * t : P * (t + 1)],
+                    rhs=moving[a][0].bitcast(FP8X4),
+                    rhs_scale=moving[a][1],
+                    start=(a == 0),
+                    stop=(a == 1),
+                )
+
+        out_rows = out_0.rearrange("(p t) m -> p t m", t=PACK)
+        out_words = out_1[0].rearrange("p m t -> p (m t)").bitcast(I32)
+
+        def y_bank(shape):
+            y_banks.append(bank("turned", 3, shape) if len(y_banks) % 5 < 3 else bank("first", 2, shape))
+            return y_banks[-1]
+
+        def make_y(c):
+            m0, width = CHUNKS[c]
+            share = 512 // width
+            y_rows[c] = row_tile(SLICES + c, [P, PACK, width])
+            for t0 in range(0, PACK, share):
+                bent_acc = y_bank([P, share, width])
+                for j in range(share):
+                    second_product(bent_acc[:, j, :], c, t0 + j, lambda a: w3_w[a], lambda a: w3_s[a])
+                bent = feature_tile()
+                nc.scalar.activation(out=bent[:], in_=bent_acc[:].rearrange("p j m -> p (j m)"), func=ACT.Tanh)
+                plain_acc = y_bank([P, share, width])
+                for j in range(share):
+                    second_product(
+                        plain_acc[:, j, :], c, t0 + j, lambda a: w4_w[:, a, :], lambda a: w4_s[4 * a : P, :]
+                    )
+                rows = y_rows[c][:, t0 : t0 + share, :]
+                nc.vector.tensor_tensor(
+                    rows.rearrange("p j m -> p (j m)"), plain_acc[:].rearrange("p j m -> p (j m)"), bent[:], ALU.add
+                )
+                nc.sync.dma_start(out=out_rows[:, t0 : t0 + share, m0 : m0 + width], in_=rows)
+
+        def weave_y(c):
+            width = CHUNKS[c][1]
+            y_stage[c] = stage_tile([P, width * PACK])
+            woven = y_stage[c][:].rearrange("p (c i t) -> p c t i", i=4, t=PACK)
+            rows = y_rows[c][:].rearrange("p t (c i) -> p c t i", i=4)
+            if c == len(CHUNKS) - 1:
+                nc.vector.tensor_copy(out=woven, in_=rows)
+            else:
+                nc.scalar.copy(out=woven, in_=rows)
+
+        def quantize_y(c):
+            m0, width = CHUNKS[c]
+            cols = slice(m0, m0 + width)
+            nc.vector.quantize_mx(out=y_w[c][:].bitcast(FP8X4), scales=y_s[:, cols], in_=y_stage[c][:])
+            nc.sync.dma_start(out=out_words[:, cols], in_=y_w[c][:].bitcast(I32))
+
+        nc.sync.dma_start(lists[1][:], offs2)
+        load_words(tab2_w[:], tab2_words[0])
+        load_w2(0)
+        nc.sync.dma_start(out=wg2_t[:], in_=wg2)
+        load_planes(tab2_s, tab2_scales)
+        nc.sync.dma_start(lists[3][:], offs4)
+        nc.sync.dma_start(lists[0][:], offs)
+        load_words(tab_w[0][:], tab_words[0])
+        load_w2(1)
+        load_planes(tab_s, tab_scales)
+        load_words(tab_w[1][:], tab_words[1])
+        load_planes(w1_s, w1_scales)
+        nc.sync.dma_start(out=w1_w[:].bitcast(I32), in_=w1_words.rearrange("a p c -> p a c").bitcast(I32))
+        nc.sync.dma_start(out=wg1_t[:], in_=wg1)
+        nc.sync.dma_start(lists[2][:], offs3)
+        nc.sync.dma_start(out=gain_t[:], in_=gain.rearrange("(g p t) -> p g t", g=2, t=PACK))
+
+        cast_w2(0)
+        load_w2(2)
+        nc.vector.tensor_copy(v2_w[:], tab2_w[:].indirect(lists[1][:]))
+        load_forecast(0)
+        nc.vector.tensor_copy(v2_s[:], tab2_s[:].indirect(lists[1][:]))
+        quantize_w2(0)
+        features_b(0)
+        nc.vector.tensor_scalar_mul(wg2_neg[:], wg2_t[:], -1.0)
+        cast_w2(1)
+        load_w2(3)
+        nc.vector.tensor_copy(v_w[0][:], tab_w[0][:].indirect(lists[0][:]))
+        place_b(0)
+        quantize_w2(1)
+        nc.vector.tensor_copy(v_w[1][:], tab_w[1][:].indirect(lists[0][:]))
+        for a in range(2):
+            nc.vector.tensor_copy(v_s[a][:], tab_s[:, T * a : T * (a + 1)].indirect(lists[0][:]))
+        features_b(1)
+        for s in range(1, 4):
+            load_forecast(s)
+        features_a(0)
+        place_b(1)
+        load_forecast(4)
+        features_a(1)
+        cast_w2(2)
+        load_w2(4)
+        place_a(0)
+        quantize_w2(2)
+        features_a(2)
+        turn_excess(0)
+        turn_placed(0)
+        place_a(1)
+        features_b(2)
+        cast_w2(3)
+        load_w3(0)
+        load_forecast(5)
+        turn_excess(1)
+        load_forecast(6)
+
+        extras = {
+            (2, 0): [lambda: quantize_w2(3), lambda: cast_w2(4), lambda: load_w3(1)],
+            (2, 1): [lambda: cast_w3(0), lambda: load_w3(2), lambda: load_forecast(7)],
+            (3, 0): [lambda: quantize_w2(4), lambda: cast_w3(1), lambda: load_w3(3)],
+            (3, 1): [lambda: cast_w3(2), load_w4],
+            (4, 0): [lambda: cast_w3(3)],
+            (4, 1): [lambda: z0_part(0, 0), lambda: z0_part(0, 1)],
+            (5, 0): [lambda: z0_part(0, 2), lambda: z0_part(0, 3)],
+            (5, 1): [lambda: z0_weave(0, 0), lambda: z0_part(1, 0)],
+            (6, 0): [lambda: z0_weave(0, 1), lambda: z0_part(1, 1)],
+            (6, 1): [lambda: z0_part(1, 2), lambda: z0_part(1, 3)],
+            (7, 0): [lambda: z0_weave(1, 0), lambda: z0_weave(1, 1)],
+            (7, 1): [],
+        }
+        for s in range(2, SLICES):
+            place_a(s)
+            if s + 1 < SLICES:
+                features_a(s + 1)
+            turn_placed(s - 1)
+            for job in extras[(s, 0)]:
+                job()
+            place_b(s)
+            if s + 1 < SLICES:
+                features_b(s + 1)
+            turn_excess(s)
+            for job in extras[(s, 1)]:
+                job()
+        for block in range(5):
+            open_z1(block)
+        turn_placed(SLICES - 1)
+
+        quantize_w3(0)
+        quantize_w3(1)
+        quantize_z0(0)
+        make_z1(0)
+        deal_w4()
+        quantize_z1(0)
+        for c in range(len(CHUNKS)):
+            if c + 1 < len(CHUNKS):
+                make_z1(c + 1)
+                quantize_z1(c + 1)
+            if c == 1:
+                quantize_z0(1)
+            make_y(c)
+            if c > 0:
+                quantize_y(c - 1)
+            weave_y(c)
+        quantize_y(len(CHUNKS) - 1)
+        for q in range(4):
+            nc.sync.dma_start(
+                out=out_2[0, 4 * q : 4 * q + 4, :].bitcast(I32), in_=y_s[32 * q : 32 * q + 4, :].bitcast(I32)
+            )

@@ -22,6 +22,9 @@ PACK = 4
 KP = P * PACK
 SLICES = H // P
 BLOCKS = T2 // P
+ROW_PLACES = [0, 8192, 20480, 4096, 12288]
+Z1_ON_VECTOR = ()
+WEAVE_ON_VECTOR = (0, 1, 2, 3, 4)
 CHUNKS = [(0, 256), (256, 256), (512, 256), (768, 128), (896, 128)]
 
 
@@ -48,11 +51,10 @@ def tile_list_sounder_bias_features_kernel(
             return work.tile(shape, BF16, name="stage", tag="stage", bufs=6, align_bytes=64)
 
         def row_tile(i, shape):
-            place = i % 5
-            return tables.tile(shape, F32, name="rows%d" % place, align_bytes=64, offset=4096 * place)
+            return tables.tile(shape, F32, name="rows%d" % i, align_bytes=64, offset=ROW_PLACES[i])
 
         def feature_tile():
-            return work.tile([P, S], F32, name="feature", tag="feature", bufs=5, align_bytes=64)
+            return work.tile([P, S], F32, name="feature", tag="feature", bufs=7, align_bytes=64)
 
         def raw_tile(shape, dtype):
             return work.tile(shape, dtype, name="raw", tag="raw", bufs=2, align_bytes=64)
@@ -80,50 +82,53 @@ def tile_list_sounder_bias_features_kernel(
             tables.tile([P, T], U32, name="tab_w%d" % a, align_bytes=64, offset=4096 + 8192 * a) for a in range(2)
         ]
         tab_s = tables.tile([P, 2 * T], U8, name="tab_s", align_bytes=64, offset=20480)
-        w4_raw_s = tables.tile([P, N], U8, name="w4_raw_s", align_bytes=64, offset=20480)
+        w4_raw_s = tables.tile([P, N], U8, name="w4_raw_s", align_bytes=64, offset=16896)
         tab2_s = held("tab2_s", [P, T3], U8)
         v_w = [held("v_w%d" % a, [P, S], U32) for a in range(2)]
         v2_w = held("v2_w", [P, S], U32)
         v2_s = held("v2_s", [P, S], U8)
         w1_w = held("w1_w", [P, 2, 2 * H], U8)
         w1_s = held("w1_s", [P, 2 * H], U8)
-        wg2_neg = laid("wg2_neg", [P, S], F32, 0)
-        last_h_b = laid("last_h_b", [P, S], F32, 2048)
+        last_wg2 = laid("last_wg2", [P, S], F32, 0)
         w3_s = [laid("w3_s%d" % a, [P, N], U8, 512 * a) for a in range(2)]
-        w4_s = laid("w4_s", [P, N], U8, 1024)
-        z0_s = [laid("z0_s0", [P, 512], U8, 1536), laid("z0_s1", [P, 512], U8, 2048)]
+        z0_s = [laid("z0_s0", [P, 512], U8, 1024), laid("z0_s1", [P, 512], U8, 8704)]
+        own_z1_stage = [laid("z1_stage%d" % c, [P, 256 * PACK], BF16, (2048, 8704)[c]) for c in range(2)]
+        w4_s = laid("w4_s", [P, N], U8, 2048)
         w4_w = laid("w4_w", [P, 2, N], U32, 2560)
         first_h_b = laid("first_h_b", [P, S], F32, 6656)
-        v_s = [laid("v_s%d" % a, [P, S], U8, 6656 + 512 * a) for a in range(2)]
-        second_h_b = tables.tile([P, S], F32, name="second_h_b", align_bytes=64, offset=19456)
-        own_h_b = {0: first_h_b, 1: second_h_b, SLICES - 1: last_h_b}
+        v_s = [laid("v_s0", [P, S], U8, 6656), tables.tile([P, S], U8, name="v_s1", align_bytes=64, offset=16384)]
+        second_h_b = tables.tile([P, S], F32, name="second_h_b", align_bytes=64, offset=12288)
+        own_h_b = {0: first_h_b, 1: second_h_b}
         w3_w = [held("w3_w%d" % a, [P, N], U32) for a in range(2)]
         wg1_t = held("wg1_t", [P, S], F32)
         wg2_t = held("wg2_t", [P, S], F32)
-        gain_t = held("gain_t", [P, 2, PACK], F32)
+        wg2_neg = held("wg2_neg", [P, S], F32)
+        gain_dealt = held("gain_dealt", [P, PACK], F32)
+        gain_rows = held("gain_rows", [P, 4], F32)
         ident = held("ident", [P, P], F32)
-        pages_a = [held("page_a%d" % i, [P, T2], F32) for i in range(2)]
-        pages_b = [held("page_b%d" % i, [P, T2], F32) for i in range(3)]
-        w2_pieces = [(0, 1), (1, 1), (2, 2), (4, 2), (6, 2)]
+        pages_a = [
+            tables.tile([P, T2], F32, name="page_a%d" % i, align_bytes=64, offset=4096 + 8192 * i) for i in range(2)
+        ]
+        pages_b = [held("page_b%d" % i, [P, T2], F32) for i in range(2)]
+        w2_pieces = [(0, 1), (1, 3), (4, 4)]
         w2_w = [held("w2_w%d" % i, [P, P * n], U32) for i, (s0, n) in enumerate(w2_pieces)]
         w2_s = [held("w2_s%d" % i, [P, P * n], U8) for i, (s0, n) in enumerate(w2_pieces)]
         z0_w = [held("z0_w%d" % h, [P, 512], U32) for h in range(2)]
-        z1_w = [held("z1_w%d" % c, [P, width], U32) for c, (m0, width) in enumerate(CHUNKS)]
-        z1_s = [held("z1_s%d" % c, [P, width], U8) for c, (m0, width) in enumerate(CHUNKS)]
+        z1_w = [held("z1_w%d" % pair, [P, 256], U32) for pair in range(4)]
+        z1_s = [held("z1_s%d" % pair, [P, 256], U8) for pair in range(4)]
         y_w = [held("y_w%d" % c, [P, width], U32) for c, (m0, width) in enumerate(CHUNKS)]
         y_s = held("y_s", [P, T2], U8)
-        excess = [[held("excess%d%d" % (g, h), [P, 4, PACK, P], F32) for h in range(2)] for g in range(2)]
-        placed = [[held("placed%d%d" % (g, h), [P, 4, PACK, P], F32) for h in range(2)] for g in range(2)]
+        excess = [laid("excess%d" % h, [P, 4, PACK, P], F32, 12288 + 8192 * h) for h in range(2)]
+        placed = [held("placed%d" % h, [P, 4, PACK, P], F32) for h in range(2)]
+        z1_turned = [held("z1_turned%d" % i, [P, 2, 2, P, 2], BF16) for i in range(4)]
 
-        zero_bytes(nc.gpsimd, tab2_s)
         for plane in (tab_s, w1_s):
             zero_bytes(nc.vector, plane)
-        nc.vector.memset(pages_b[0][:], 0.0)
-        for page in (pages_b[1], pages_a[0], pages_a[1], pages_b[2]):
-            nc.gpsimd.memset(page[:], 0.0)
+        for page in pages_b:
+            nc.vector.memset(page[:], 0.0)
         make_identity(nc, ident[:])
 
-        z1_acc, w4_raw, y_banks = {}, {}, []
+        z1_acc, w4_raw, peak, weight_b, y_banks = {}, {}, {}, {}, []
         w2_raw, w3_raw, w2_stage, w3_stage, f_rows = {}, {}, {}, {}, {}
         h_a, h_b, z0_rows, z0_stage, z1_stage, y_rows, y_stage = {}, {}, {}, {}, {}, {}, {}
 
@@ -143,13 +148,9 @@ def tile_list_sounder_bias_features_kernel(
         def quantize_w2(i):
             nc.vector.quantize_mx(out=w2_w[i][:].bitcast(FP8X4), scales=w2_s[i][:], in_=w2_stage[i][:])
 
-        def load_w3(i):
-            a, half = divmod(i, 2)
-            w3_raw[i] = raw_tile([P, PACK, 256], F32)
-            nc.sync.dma_start(
-                out=w3_raw[i][:],
-                in_=w3[KP * a : KP * (a + 1), 256 * half : 256 * (half + 1)].rearrange("(p j) c -> p j c", j=PACK),
-            )
+        def load_w3(a):
+            w3_raw[a] = raw_tile([P, PACK, N], F32)
+            nc.sync.dma_start(out=w3_raw[a][:], in_=w3[KP * a : KP * (a + 1), :].rearrange("(p j) c -> p j c", j=PACK))
 
         def cast_w3(i):
             a, half = divmod(i, 2)
@@ -157,7 +158,7 @@ def tile_list_sounder_bias_features_kernel(
                 w3_stage[a] = stage_tile([P, PACK, P, PACK])
             nc.scalar.copy(
                 out=w3_stage[a][:, :, 64 * half : 64 * (half + 1), :].rearrange("p t q j -> p q j t"),
-                in_=w3_raw[i][:].rearrange("p j (q t) -> p q j t", t=PACK),
+                in_=w3_raw[a][:, :, 256 * half : 256 * (half + 1)].rearrange("p j (q t) -> p q j t", t=PACK),
             )
 
         def quantize_w3(a):
@@ -188,7 +189,7 @@ def tile_list_sounder_bias_features_kernel(
             )
 
         def load_forecast(s):
-            f_rows[s] = row_tile(s, [P, T2])
+            f_rows[s] = row_tile(s % 3, [P, T2])
             nc.sync.dma_start(out=f_rows[s][:], in_=forecast[P * s : P * (s + 1), :])
 
         def features_a(s):
@@ -204,7 +205,7 @@ def tile_list_sounder_bias_features_kernel(
                     stop=(a == 1),
                 )
             h_a[s] = feature_tile()
-            nc.scalar.activation(out=h_a[s][:], in_=acc[:], func=ACT.Tanh, scale=-1.0)
+            nc.scalar.activation(out=h_a[s][:], in_=acc[:], func=ACT.Tanh, scale=(-1.0 if s < 4 else 1.0))
 
         def features_b(s):
             i = max(j for j, (s0, n) in enumerate(w2_pieces) if s0 <= s)
@@ -222,53 +223,93 @@ def tile_list_sounder_bias_features_kernel(
             h_b[s] = own_h_b[s] if s in own_h_b else feature_tile()
             nc.scalar.activation(out=h_b[s][:], in_=acc[:], func=ACT.Silu)
 
+        def weigh_b(s):
+            weight_b[s] = wg2_neg
+            if s >= 4:
+                weight_b[s] = last_wg2 if s == SLICES - 1 else feature_tile()
+                nc.scalar.activation(
+                    out=weight_b[s][:], in_=wg2_t[:], func=ACT.Copy, scale=gain_rows[:, s - 4 : s - 3]
+                )
+
         def place_a(s):
             nc.vector.tensor_tensor(pages_a[s % 2][:].indirect(lists[2][:]), h_a[s][:], wg1_t[:], ALU.mult)
 
         def place_b(s):
-            nc.vector.tensor_tensor(pages_b[s % 3][:].indirect(lists[3][:]), h_b[s][:], wg2_neg[:], ALU.mult)
+            nc.vector.tensor_tensor(pages_b[s % 2][:].indirect(lists[3][:]), h_b[s][:], weight_b[s][:], ALU.mult)
 
         def add_turned(out, first, second):
             nc.tensor.matmul(out, lhsT=first, rhs=ident[:], start=True, stop=False, is_transpose=True)
             nc.tensor.matmul(out, lhsT=second, rhs=ident[:], start=False, stop=True, is_transpose=True)
 
-        def turn_sum(s, first, second, dest, func, scale, blocks):
-            g, quarter = divmod(s, 4)
-            for b0 in range(0, BLOCKS, blocks):
-                acc = bank("turned", 3, [P, blocks, P])
-                for b in range(blocks):
-                    cols = slice(P * (b0 + b), P * (b0 + b + 1))
-                    add_turned(acc[:, b, :], first[:, cols], second[:, cols])
-                half, b1 = divmod(b0, 4)
+        def block_of(tile, b):
+            return tile[:, P * b : P * (b + 1)]
+
+        def turn_sum(s, first, second, dest, func, scale):
+            for half in range(2):
+                acc = bank("turned", 3, [P, 4, P])
+                for b in range(4):
+                    add_turned(acc[:, b, :], block_of(first, 4 * half + b), block_of(second, 4 * half + b))
                 nc.scalar.activation(
-                    out=dest[g][half][:, b1 : b1 + blocks, :, 32 * quarter : 32 * (quarter + 1)],
+                    out=dest[half][:, :, :, 32 * s : 32 * (s + 1)],
                     in_=acc[:].rearrange("m b (p t) -> m b t p", t=PACK),
                     func=func,
                     scale=scale,
                 )
 
         def turn_excess(s):
-            turn_sum(s, f_rows[s], pages_a[s % 2], excess, ACT.Relu, 1.0, 4)
+            turn_sum(s, f_rows[s], pages_a[s % 2], excess, ACT.Relu, 1.0)
 
         def turn_placed(s):
-            turn_sum(s, pages_a[s % 2], pages_b[s % 3], placed, ACT.Copy, -1.0, 2 if s == SLICES - 1 else 4)
+            turn_sum(s, pages_a[s % 2], pages_b[s % 2], placed, ACT.Copy, -1.0)
+
+        def make_peak(s):
+            plain = laid("plain_peak%d" % (s % 2), [P, T2], F32, 28672 + 4096 * (s % 2))
+            nc.vector.tensor_tensor(plain[:], pages_a[s % 2][:], f_rows[s][:], ALU.max)
+            peak[s] = laid("peak%d" % min(s, 5), [P, T2], F32, 12288 + 8192 * (min(s, 5) - 4))
+            nc.scalar.activation(out=peak[s][:], in_=plain[:], func=ACT.Copy, scale=gain_rows[:, s - 4 : s - 3])
+
+        def round_z1(s, pair, acc):
+            quarter = s - 4
+            nc.scalar.copy(
+                out=z1_turned[pair][:, :, :, 32 * quarter : 32 * (quarter + 1), :],
+                in_=acc.rearrange("m b (p u e) -> m b u p e", u=2, e=2),
+            )
+
+        def turn_z1(s):
+            for half in range(2):
+                acc = bank("turned", 3, [P, 4, P])
+                for b in range(4):
+                    add_turned(acc[:, b, :], block_of(peak[s], 4 * half + b), block_of(pages_b[s % 2], 4 * half + b))
+                for j in range(2):
+                    round_z1(s, 2 * half + j, acc[:, 2 * j : 2 * j + 2, :])
+
+        def turn_pair(pair, source, opens):
+            for j in range(2):
+                nc.tensor.matmul(
+                    z1_acc[pair][:, j, :],
+                    lhsT=block_of(source, 2 * pair + j),
+                    rhs=ident[:],
+                    start=(opens and j == 0),
+                    stop=(not opens and j == 1),
+                    is_transpose=True,
+                )
 
         def z0_part(half, t):
             if t == 0:
                 z0_rows[half] = stage_tile([P, PACK, 512])
             acc = bank("back", 3, [P, 4, P])
             for b in range(4):
-                add_turned(acc[:, b, :], excess[0][half][:, b, t, :], placed[0][half][:, b, t, :])
+                add_turned(acc[:, b, :], excess[half][:, b, t, :], placed[half][:, b, t, :])
             nc.scalar.activation(
                 out=z0_rows[half][:, t, :],
                 in_=acc[:].rearrange("p b m -> p (b m)"),
                 func=ACT.Copy,
-                scale=gain_t[:, 0, t : t + 1],
+                scale=gain_dealt[:, t : t + 1],
             )
 
         def z0_weave(half, part):
             if part == 0:
-                z0_stage[half] = stage_tile([P, 512 * PACK])
+                z0_stage[half] = stage_tile([P, 512 * PACK]) if half == 0 else laid("z0_stage1", [P, 512 * PACK], BF16, 28672)
             nc.scalar.copy(
                 out=z0_stage[half][:, 1024 * part : 1024 * (part + 1)].rearrange("p (c i t) -> p c t i", i=4, t=PACK),
                 in_=z0_rows[half][:, :, 256 * part : 256 * (part + 1)].rearrange("p t (c i) -> p c t i", i=4),
@@ -277,48 +318,29 @@ def tile_list_sounder_bias_features_kernel(
         def quantize_z0(half):
             nc.vector.quantize_mx(out=z0_w[half][:].bitcast(FP8X4), scales=z0_s[half][:], in_=z0_stage[half][:])
 
-        def turn_back(acc, source, block, opens):
-            half, b = divmod(block, 4)
-            for t in range(PACK):
-                nc.tensor.matmul(
-                    acc[:, t, :],
-                    lhsT=source[1][half][:, b, t, :],
-                    rhs=ident[:],
-                    start=(opens and t == 0),
-                    stop=(not opens and t == PACK - 1),
-                    is_transpose=True,
-                )
-
-        def open_z1(block):
-            z1_acc[block] = bank("first", 2, [P, PACK, P]) if block in (3, 4) else bank("back", 3, [P, PACK, P])
-            turn_back(z1_acc[block], excess, block, True)
-
         def make_z1(c):
-            m0, width = CHUNKS[c]
-            z1_stage[c] = stage_tile([P, width // P, P, PACK])
-            for j in range(width // P):
-                block = m0 // P + j
-                if block not in z1_acc:
-                    open_z1(block)
-                acc = z1_acc[block]
-                turn_back(acc, placed, block, False)
-                nc.vector.tensor_tensor(
-                    z1_stage[c][:, j, :, :],
-                    acc[:].rearrange("p t m -> p m t"),
-                    gain_t[:, 1, :].unsqueeze(1).to_broadcast([P, P, PACK]),
-                    ALU.mult,
-                )
+            z1_stage[c] = own_z1_stage[c] if c < 2 else stage_tile([P, 256 * PACK])
+            acc = bank("back", 3, [P, 2, 2, P]) if c < 3 else bank("first", 2, [P, 2, 2, P])
+            for b in range(2):
+                for u in range(2):
+                    words = z1_turned[c][:, b, u, :, :].rearrange("m p e -> m (p e)").bitcast(F32)
+                    nc.tensor.transpose(acc[:, b, u, :], words, ident[:])
+            woven = z1_stage[c][:].bitcast(F32).rearrange("p (b m u) -> p b m u", b=2, u=2)
+            if c in Z1_ON_VECTOR:
+                nc.vector.tensor_copy(out=woven, in_=acc[:].rearrange("p b u m -> p b m u"))
+            else:
+                nc.scalar.copy(out=woven, in_=acc[:].rearrange("p b u m -> p b m u"))
 
         def quantize_z1(c):
-            nc.vector.quantize_mx(
-                out=z1_w[c][:].bitcast(FP8X4), scales=z1_s[c][:], in_=z1_stage[c][:].rearrange("p j m t -> p (j m t)")
-            )
+            nc.vector.quantize_mx(out=z1_w[c][:].bitcast(FP8X4), scales=z1_s[c][:], in_=z1_stage[c][:])
 
         def second_product(acc, c, t, weight_words, weight_scales):
             m0, width = CHUNKS[c]
             half, first = divmod(m0, 512)
             cols = slice(first, first + width)
-            moving = [(z0_w[half][:, cols], z0_s[half][:, cols]), (z1_w[c][:], z1_s[c][:])]
+            pair, start = divmod(m0, 256)
+            near = slice(start, start + width)
+            moving = [(z0_w[half][:, cols], z0_s[half][:, cols]), (z1_w[pair][:, near], z1_s[pair][:, near])]
             for a in range(2):
                 nc.tensor.matmul_mx(
                     out=acc,
@@ -334,13 +356,14 @@ def tile_list_sounder_bias_features_kernel(
         out_words = out_1[0].rearrange("p m t -> p (m t)").bitcast(I32)
 
         def y_bank(shape):
-            y_banks.append(bank("turned", 3, shape) if len(y_banks) % 5 < 3 else bank("first", 2, shape))
+            tag, bufs = ([("turned", 3)] * 3 + [("first", 2)] * 2 + [("back", 3)] * 3)[len(y_banks) % 8]
+            y_banks.append(bank(tag, bufs, shape))
             return y_banks[-1]
 
         def make_y(c):
             m0, width = CHUNKS[c]
             share = 512 // width
-            y_rows[c] = row_tile(SLICES + c, [P, PACK, width])
+            y_rows[c] = row_tile((c + 3) % 5, [P, PACK, width])
             for t0 in range(0, PACK, share):
                 bent_acc = y_bank([P, share, width])
                 for j in range(share):
@@ -363,7 +386,7 @@ def tile_list_sounder_bias_features_kernel(
             y_stage[c] = stage_tile([P, width * PACK])
             woven = y_stage[c][:].rearrange("p (c i t) -> p c t i", i=4, t=PACK)
             rows = y_rows[c][:].rearrange("p t (c i) -> p c t i", i=4)
-            if c == len(CHUNKS) - 1:
+            if c in WEAVE_ON_VECTOR:
                 nc.vector.tensor_copy(out=woven, in_=rows)
             else:
                 nc.scalar.copy(out=woven, in_=rows)
@@ -376,102 +399,127 @@ def tile_list_sounder_bias_features_kernel(
 
         nc.sync.dma_start(lists[1][:], offs2)
         load_words(tab2_w[:], tab2_words[0])
+        for q in range(4):
+            nc.sync.dma_start(
+                out=tab2_s[32 * q : 32 * (q + 1), :].bitcast(I32),
+                in_=tab2_scales[0, 4 * q : 4 * q + 4, :].bitcast(I32).unsqueeze(0).to_broadcast([8, 4, T3 // 4]),
+            )
         load_w2(0)
         nc.sync.dma_start(out=wg2_t[:], in_=wg2)
-        load_planes(tab2_s, tab2_scales)
-        nc.sync.dma_start(lists[3][:], offs4)
-        nc.sync.dma_start(lists[0][:], offs)
         load_words(tab_w[0][:], tab_words[0])
+        nc.sync.dma_start(lists[0][:], offs)
+        nc.sync.dma_start(lists[3][:], offs4)
         load_w2(1)
-        load_planes(tab_s, tab_scales)
         load_words(tab_w[1][:], tab_words[1])
-        load_planes(w1_s, w1_scales)
+        load_planes(tab_s, tab_scales)
         nc.sync.dma_start(out=w1_w[:].bitcast(I32), in_=w1_words.rearrange("a p c -> p a c").bitcast(I32))
+        load_planes(w1_s, w1_scales)
         nc.sync.dma_start(out=wg1_t[:], in_=wg1)
         nc.sync.dma_start(lists[2][:], offs3)
-        nc.sync.dma_start(out=gain_t[:], in_=gain.rearrange("(g p t) -> p g t", g=2, t=PACK))
+        nc.sync.dma_start(out=gain_dealt[:], in_=gain[0:KP].rearrange("(p t) -> p t", t=PACK))
+        with nc.allow_non_contiguous_dma(reason="one gain for each partition and slice"):
+            nc.sync.dma_start(out=gain_rows[:], in_=gain[KP:H].rearrange("(s p) -> p s", p=P))
 
         cast_w2(0)
-        load_w2(2)
         nc.vector.tensor_copy(v2_w[:], tab2_w[:].indirect(lists[1][:]))
-        load_forecast(0)
         nc.vector.tensor_copy(v2_s[:], tab2_s[:].indirect(lists[1][:]))
         quantize_w2(0)
         features_b(0)
         nc.vector.tensor_scalar_mul(wg2_neg[:], wg2_t[:], -1.0)
+        for s in range(4):
+            weigh_b(s)
         cast_w2(1)
-        load_w2(3)
+        load_forecast(0)
+        load_w2(2)
         nc.vector.tensor_copy(v_w[0][:], tab_w[0][:].indirect(lists[0][:]))
+        nc.gpsimd.memset(pages_a[0][:], 0.0)
         place_b(0)
         quantize_w2(1)
         nc.vector.tensor_copy(v_w[1][:], tab_w[1][:].indirect(lists[0][:]))
         for a in range(2):
             nc.vector.tensor_copy(v_s[a][:], tab_s[:, T * a : T * (a + 1)].indirect(lists[0][:]))
         features_b(1)
-        for s in range(1, 4):
-            load_forecast(s)
+        load_forecast(1)
+        load_w3(0)
+        load_forecast(2)
         features_a(0)
         place_b(1)
-        load_forecast(4)
+        nc.gpsimd.memset(pages_a[1][:], 0.0)
         features_a(1)
         cast_w2(2)
-        load_w2(4)
+        load_w3(1)
         place_a(0)
-        quantize_w2(2)
         features_a(2)
+        features_b(2)
         turn_excess(0)
+        load_forecast(3)
         turn_placed(0)
         place_a(1)
-        features_b(2)
-        cast_w2(3)
-        load_w3(0)
-        load_forecast(5)
+        quantize_w2(2)
+        cast_w3(0)
+        cast_w3(1)
+        load_w4()
         turn_excess(1)
-        load_forecast(6)
+        load_forecast(4)
 
         extras = {
-            (2, 0): [lambda: quantize_w2(3), lambda: cast_w2(4), lambda: load_w3(1)],
-            (2, 1): [lambda: cast_w3(0), lambda: load_w3(2), lambda: load_forecast(7)],
-            (3, 0): [lambda: quantize_w2(4), lambda: cast_w3(1), lambda: load_w3(3)],
-            (3, 1): [lambda: cast_w3(2), load_w4],
-            (4, 0): [lambda: cast_w3(3)],
-            (4, 1): [lambda: z0_part(0, 0), lambda: z0_part(0, 1)],
-            (5, 0): [lambda: z0_part(0, 2), lambda: z0_part(0, 3)],
-            (5, 1): [lambda: z0_weave(0, 0), lambda: z0_part(1, 0)],
-            (6, 0): [lambda: z0_weave(0, 1), lambda: z0_part(1, 1)],
-            (6, 1): [lambda: z0_part(1, 2), lambda: z0_part(1, 3)],
+            (2, 0): [lambda: cast_w3(2)],
+            (2, 1): [lambda: cast_w3(3)],
+            (3, 0): [lambda: weigh_b(4)],
+            (3, 1): [],
+            (4, 0): [lambda: weigh_b(5), lambda: z0_part(0, 0), lambda: z0_part(0, 1), lambda: z0_part(0, 2), lambda: z0_part(0, 3)],
+            (4, 1): [],
+            (5, 0): [lambda: weigh_b(6), lambda: z0_part(1, 0), lambda: z0_part(1, 1), lambda: z0_part(1, 2), lambda: z0_part(1, 3)],
+            (5, 1): [],
+            (6, 0): [lambda: weigh_b(7), lambda: z0_weave(0, 0), lambda: z0_weave(0, 1)],
+            (6, 1): [],
             (7, 0): [lambda: z0_weave(1, 0), lambda: z0_weave(1, 1)],
             (7, 1): [],
         }
         for s in range(2, SLICES):
+            last = s == SLICES - 1
             place_a(s)
-            if s + 1 < SLICES:
+            if not last:
                 features_a(s + 1)
-            turn_placed(s - 1)
+                features_b(s + 1)
+            if s - 1 < 4:
+                turn_placed(s - 1)
+            else:
+                turn_z1(s - 1)
             for job in extras[(s, 0)]:
                 job()
+            if last:
+                make_peak(s)
             place_b(s)
-            if s + 1 < SLICES:
-                features_b(s + 1)
-            turn_excess(s)
+            if s < 4:
+                turn_excess(s)
+            elif not last:
+                make_peak(s)
+            if s + 3 < SLICES:
+                load_forecast(s + 3)
             for job in extras[(s, 1)]:
                 job()
-        for block in range(5):
-            open_z1(block)
-        turn_placed(SLICES - 1)
+        last = SLICES - 1
+        for pair in range(4):
+            z1_acc[pair] = bank("turned", 3, [P, 2, P]) if pair < 3 else bank("first", 2, [P, 2, P])
+            turn_pair(pair, peak[last], True)
+        for pair in range(4):
+            turn_pair(pair, pages_b[last % 2], False)
+            round_z1(last, pair, z1_acc[pair][:])
 
         quantize_w3(0)
         quantize_w3(1)
         quantize_z0(0)
         make_z1(0)
-        deal_w4()
         quantize_z1(0)
+        deal_w4()
+        make_z1(1)
+        quantize_z1(1)
+        quantize_z0(1)
+        for c in range(2, 4):
+            make_z1(c)
+            quantize_z1(c)
         for c in range(len(CHUNKS)):
-            if c + 1 < len(CHUNKS):
-                make_z1(c + 1)
-                quantize_z1(c + 1)
-            if c == 1:
-                quantize_z0(1)
             make_y(c)
             if c > 0:
                 quantize_y(c - 1)

@@ -22,10 +22,18 @@ PACK = 4
 KP = P * PACK
 SLICES = H // P
 BLOCKS = T2 // P
-ROW_PLACES = [0, 8192, 20480, 4096, 12288]
+ROW_PLACES = [0, 8192, 26624]
+Y_PLACES = [4096, 22528, 18432, 26624, 28672]
+WEAVE_ON_SCALAR = ()
 Z1_ON_VECTOR = ()
-WEAVE_ON_VECTOR = (0, 1, 2, 3, 4)
 CHUNKS = [(0, 256), (256, 256), (512, 256), (768, 128), (896, 128)]
+EARLY = [(0, 0), (0, 2), (1, 0), (1, 2)]
+LAST_BANKS = [(0, 2), (2, 4), (6, 2)]
+Y_BANKS = [
+    ["first", "back", "first", "turned"], ["back", "turned", "back", "first"], ["first", "turned", "back", "turned"],
+    ["back", "first"], ["back", "first"],
+]
+BANK_BUFS = {"first": 2, "turned": 3, "back": 3}
 
 
 def tile_list_sounder_bias_features_kernel(
@@ -57,7 +65,7 @@ def tile_list_sounder_bias_features_kernel(
             return work.tile([P, S], F32, name="feature", tag="feature", bufs=7, align_bytes=64)
 
         def raw_tile(shape, dtype):
-            return work.tile(shape, dtype, name="raw", tag="raw", bufs=2, align_bytes=64)
+            return work.tile(shape, dtype, name="raw", tag="raw", bufs=3, align_bytes=64)
 
         def bank(tag, bufs, shape):
             return psum.tile(shape, F32, name=tag, tag=tag, bufs=bufs)
@@ -82,22 +90,21 @@ def tile_list_sounder_bias_features_kernel(
             tables.tile([P, T], U32, name="tab_w%d" % a, align_bytes=64, offset=4096 + 8192 * a) for a in range(2)
         ]
         tab_s = tables.tile([P, 2 * T], U8, name="tab_s", align_bytes=64, offset=20480)
-        w4_raw_s = tables.tile([P, N], U8, name="w4_raw_s", align_bytes=64, offset=16896)
+        w4_raw_s = tables.tile([P, N], U8, name="w4_raw_s", align_bytes=64, offset=13312)
         tab2_s = held("tab2_s", [P, T3], U8)
-        v_w = [held("v_w%d" % a, [P, S], U32) for a in range(2)]
+        v_w = [held("v_w0", [P, S], U32), laid("v_w1", [P, S], U32, 10240)]
         v2_w = held("v2_w", [P, S], U32)
         v2_s = held("v2_s", [P, S], U8)
         w1_w = held("w1_w", [P, 2, 2 * H], U8)
         w1_s = held("w1_s", [P, 2 * H], U8)
         last_wg2 = laid("last_wg2", [P, S], F32, 0)
-        w3_s = [laid("w3_s%d" % a, [P, N], U8, 512 * a) for a in range(2)]
-        z0_s = [laid("z0_s0", [P, 512], U8, 1024), laid("z0_s1", [P, 512], U8, 8704)]
-        own_z1_stage = [laid("z1_stage%d" % c, [P, 256 * PACK], BF16, (2048, 8704)[c]) for c in range(2)]
-        w4_s = laid("w4_s", [P, N], U8, 2048)
-        w4_w = laid("w4_w", [P, 2, N], U32, 2560)
-        first_h_b = laid("first_h_b", [P, S], F32, 6656)
-        v_s = [laid("v_s0", [P, S], U8, 6656), tables.tile([P, S], U8, name="v_s1", align_bytes=64, offset=16384)]
-        second_h_b = tables.tile([P, S], F32, name="second_h_b", align_bytes=64, offset=12288)
+        w3_s = [tables.tile([P, N], U8, name="w3_s0", align_bytes=64, offset=0), laid("w3_s1", [P, N], U8, 0)]
+        z0_s = [laid("z0_s0", [P, 512], U8, 20480), laid("z0_s1", [P, 512], U8, 512)]
+        w4_s = laid("w4_s", [P, N], U8, 1024)
+        w4_w = laid("w4_w", [P, 2, N], U32, 1536)
+        first_h_b = laid("first_h_b", [P, S], F32, 10240)
+        v_s = [tables.tile([P, S], U8, name="v_s%d" % a, align_bytes=64, offset=12288 + 512 * a) for a in range(2)]
+        second_h_b = tables.tile([P, S], F32, name="second_h_b", align_bytes=64, offset=13312)
         own_h_b = {0: first_h_b, 1: second_h_b}
         w3_w = [held("w3_w%d" % a, [P, N], U32) for a in range(2)]
         wg1_t = held("wg1_t", [P, S], F32)
@@ -107,7 +114,7 @@ def tile_list_sounder_bias_features_kernel(
         gain_rows = held("gain_rows", [P, 4], F32)
         ident = held("ident", [P, P], F32)
         pages_a = [
-            tables.tile([P, T2], F32, name="page_a%d" % i, align_bytes=64, offset=4096 + 8192 * i) for i in range(2)
+            tables.tile([P, T2], F32, name="page_a%d" % i, align_bytes=64, offset=(4096, 18432, 22528)[i]) for i in range(3)
         ]
         pages_b = [held("page_b%d" % i, [P, T2], F32) for i in range(2)]
         w2_pieces = [(0, 1), (1, 3), (4, 4)]
@@ -124,11 +131,11 @@ def tile_list_sounder_bias_features_kernel(
 
         for plane in (tab_s, w1_s):
             zero_bytes(nc.vector, plane)
-        for page in pages_b:
-            nc.vector.memset(page[:], 0.0)
+        nc.vector.memset(pages_b[0][:], 0.0)
         make_identity(nc, ident[:])
+        nc.gpsimd.memset(pages_b[1][:], 0.0)
 
-        z1_acc, w4_raw, peak, weight_b, y_banks = {}, {}, {}, {}, []
+        z1_acc, w4_raw, peak, weight_b, y_acc = {}, {}, {}, {}, {}
         w2_raw, w3_raw, w2_stage, w3_stage, f_rows = {}, {}, {}, {}, {}
         h_a, h_b, z0_rows, z0_stage, z1_stage, y_rows, y_stage = {}, {}, {}, {}, {}, {}, {}
 
@@ -226,13 +233,13 @@ def tile_list_sounder_bias_features_kernel(
         def weigh_b(s):
             weight_b[s] = wg2_neg
             if s >= 4:
-                weight_b[s] = last_wg2 if s == SLICES - 1 else feature_tile()
+                weight_b[s] = last_wg2 if s == SLICES - 1 else held("wg2_gain%d" % s, [P, S], F32)
                 nc.scalar.activation(
                     out=weight_b[s][:], in_=wg2_t[:], func=ACT.Copy, scale=gain_rows[:, s - 4 : s - 3]
                 )
 
         def place_a(s):
-            nc.vector.tensor_tensor(pages_a[s % 2][:].indirect(lists[2][:]), h_a[s][:], wg1_t[:], ALU.mult)
+            nc.vector.tensor_tensor(pages_a[s % 3][:].indirect(lists[2][:]), h_a[s][:], wg1_t[:], ALU.mult)
 
         def place_b(s):
             nc.vector.tensor_tensor(pages_b[s % 2][:].indirect(lists[3][:]), h_b[s][:], weight_b[s][:], ALU.mult)
@@ -257,15 +264,15 @@ def tile_list_sounder_bias_features_kernel(
                 )
 
         def turn_excess(s):
-            turn_sum(s, f_rows[s], pages_a[s % 2], excess, ACT.Relu, 1.0)
+            turn_sum(s, f_rows[s], pages_a[s % 3], excess, ACT.Relu, 1.0)
 
         def turn_placed(s):
-            turn_sum(s, pages_a[s % 2], pages_b[s % 2], placed, ACT.Copy, -1.0)
+            turn_sum(s, pages_a[s % 3], pages_b[s % 2], placed, ACT.Copy, -1.0)
 
         def make_peak(s):
-            plain = laid("plain_peak%d" % (s % 2), [P, T2], F32, 28672 + 4096 * (s % 2))
-            nc.vector.tensor_tensor(plain[:], pages_a[s % 2][:], f_rows[s][:], ALU.max)
-            peak[s] = laid("peak%d" % min(s, 5), [P, T2], F32, 12288 + 8192 * (min(s, 5) - 4))
+            plain = laid("plain_peak%d" % s, [P, T2], F32, (28672, 32768, 28672, 2048)[s - 4])
+            nc.vector.tensor_tensor(plain[:], pages_a[s % 3][:], f_rows[s][:], ALU.max)
+            peak[s] = laid("peak%d" % s, [P, T2], F32, (12288, 20480, 20480, 22528)[s - 4])
             nc.scalar.activation(out=peak[s][:], in_=plain[:], func=ACT.Copy, scale=gain_rows[:, s - 4 : s - 3])
 
         def round_z1(s, pair, acc):
@@ -283,14 +290,15 @@ def tile_list_sounder_bias_features_kernel(
                 for j in range(2):
                     round_z1(s, 2 * half + j, acc[:, 2 * j : 2 * j + 2, :])
 
-        def turn_pair(pair, source, opens):
-            for j in range(2):
+        def turn_blocks(g, source, opens):
+            b0, n = LAST_BANKS[g]
+            for j in range(n):
                 nc.tensor.matmul(
-                    z1_acc[pair][:, j, :],
-                    lhsT=block_of(source, 2 * pair + j),
+                    z1_acc[g][:, j, :],
+                    lhsT=block_of(source, b0 + j),
                     rhs=ident[:],
                     start=(opens and j == 0),
-                    stop=(not opens and j == 1),
+                    stop=(not opens and j == n - 1),
                     is_transpose=True,
                 )
 
@@ -308,19 +316,24 @@ def tile_list_sounder_bias_features_kernel(
             )
 
         def z0_weave(half, part):
-            if part == 0:
-                z0_stage[half] = stage_tile([P, 512 * PACK]) if half == 0 else laid("z0_stage1", [P, 512 * PACK], BF16, 28672)
+            z0_stage[half, part] = laid(
+                "z0_stage%d%d" % (half, part), [P, 256 * PACK], BF16, ((0, 2048), (28672, 5632))[half][part]
+            )
             nc.scalar.copy(
-                out=z0_stage[half][:, 1024 * part : 1024 * (part + 1)].rearrange("p (c i t) -> p c t i", i=4, t=PACK),
+                out=z0_stage[half, part][:].rearrange("p (c i t) -> p c t i", i=4, t=PACK),
                 in_=z0_rows[half][:, :, 256 * part : 256 * (part + 1)].rearrange("p t (c i) -> p c t i", i=4),
             )
 
         def quantize_z0(half):
-            nc.vector.quantize_mx(out=z0_w[half][:].bitcast(FP8X4), scales=z0_s[half][:], in_=z0_stage[half][:])
+            for part in range(2):
+                cols = slice(256 * part, 256 * (part + 1))
+                nc.vector.quantize_mx(
+                    out=z0_w[half][:, cols].bitcast(FP8X4), scales=z0_s[half][:, cols], in_=z0_stage[half, part][:]
+                )
 
         def make_z1(c):
-            z1_stage[c] = own_z1_stage[c] if c < 2 else stage_tile([P, 256 * PACK])
-            acc = bank("back", 3, [P, 2, 2, P]) if c < 3 else bank("first", 2, [P, 2, 2, P])
+            z1_stage[c] = stage_tile([P, 256 * PACK])
+            acc = bank("turned", 3, [P, 2, 2, P])
             for b in range(2):
                 for u in range(2):
                     words = z1_turned[c][:, b, u, :, :].rearrange("m p e -> m (p e)").bitcast(F32)
@@ -334,50 +347,52 @@ def tile_list_sounder_bias_features_kernel(
         def quantize_z1(c):
             nc.vector.quantize_mx(out=z1_w[c][:].bitcast(FP8X4), scales=z1_s[c][:], in_=z1_stage[c][:])
 
-        def second_product(acc, c, t, weight_words, weight_scales):
+        def second_pass(c, g, a):
             m0, width = CHUNKS[c]
-            half, first = divmod(m0, 512)
+            share = 512 // width
+            t0 = share * (g // 2)
+            if a == 0:
+                tag = Y_BANKS[c][g]
+                y_acc[c, g] = bank(tag, BANK_BUFS[tag], [P, share, width])
+                half, first = divmod(m0, 512)
+                words, scales = z0_w[half], z0_s[half]
+            else:
+                pair, first = divmod(m0, 256)
+                words, scales = z1_w[pair], z1_s[pair]
             cols = slice(first, first + width)
-            pair, start = divmod(m0, 256)
-            near = slice(start, start + width)
-            moving = [(z0_w[half][:, cols], z0_s[half][:, cols]), (z1_w[pair][:, near], z1_s[pair][:, near])]
-            for a in range(2):
+            for j in range(share):
+                rows = slice(P * (t0 + j), P * (t0 + j + 1))
                 nc.tensor.matmul_mx(
-                    out=acc,
-                    lhsT=weight_words(a)[:, P * t : P * (t + 1)].bitcast(FP8X4),
-                    lhsT_scale=weight_scales(a)[:, P * t : P * (t + 1)],
-                    rhs=moving[a][0].bitcast(FP8X4),
-                    rhs_scale=moving[a][1],
-                    start=(a == 0),
-                    stop=(a == 1),
+                    out=y_acc[c, g][:, j, :],
+                    lhsT=(w4_w[:, a, rows] if g % 2 else w3_w[a][:, rows]).bitcast(FP8X4),
+                    lhsT_scale=w4_s[4 * a : P, rows] if g % 2 else w3_s[a][:, rows],
+                    rhs=words[:, cols].bitcast(FP8X4),
+                    rhs_scale=scales[:, cols],
+                    start=(a == 0 and j == 0),
+                    stop=(a == 1 and j == share - 1),
                 )
+
+        def finish_sum(c, g):
+            if (c, g) not in EARLY:
+                second_pass(c, g, 0)
+            second_pass(c, g, 1)
 
         out_rows = out_0.rearrange("(p t) m -> p t m", t=PACK)
         out_words = out_1[0].rearrange("p m t -> p (m t)").bitcast(I32)
 
-        def y_bank(shape):
-            tag, bufs = ([("turned", 3)] * 3 + [("first", 2)] * 2 + [("back", 3)] * 3)[len(y_banks) % 8]
-            y_banks.append(bank(tag, bufs, shape))
-            return y_banks[-1]
-
         def make_y(c):
             m0, width = CHUNKS[c]
             share = 512 // width
-            y_rows[c] = row_tile((c + 3) % 5, [P, PACK, width])
-            for t0 in range(0, PACK, share):
-                bent_acc = y_bank([P, share, width])
-                for j in range(share):
-                    second_product(bent_acc[:, j, :], c, t0 + j, lambda a: w3_w[a], lambda a: w3_s[a])
+            y_rows[c] = tables.tile([P, PACK, width], F32, name="y_rows%d" % c, align_bytes=64, offset=Y_PLACES[c])
+            for g in range(0, 2 * PACK // share, 2):
+                t0 = share * (g // 2)
+                finish_sum(c, g)
                 bent = feature_tile()
-                nc.scalar.activation(out=bent[:], in_=bent_acc[:].rearrange("p j m -> p (j m)"), func=ACT.Tanh)
-                plain_acc = y_bank([P, share, width])
-                for j in range(share):
-                    second_product(
-                        plain_acc[:, j, :], c, t0 + j, lambda a: w4_w[:, a, :], lambda a: w4_s[4 * a : P, :]
-                    )
+                nc.scalar.activation(out=bent[:], in_=y_acc[c, g][:].rearrange("p j m -> p (j m)"), func=ACT.Tanh)
+                finish_sum(c, g + 1)
                 rows = y_rows[c][:, t0 : t0 + share, :]
                 nc.vector.tensor_tensor(
-                    rows.rearrange("p j m -> p (j m)"), plain_acc[:].rearrange("p j m -> p (j m)"), bent[:], ALU.add
+                    rows.rearrange("p j m -> p (j m)"), y_acc[c, g + 1][:].rearrange("p j m -> p (j m)"), bent[:], ALU.add
                 )
                 nc.sync.dma_start(out=out_rows[:, t0 : t0 + share, m0 : m0 + width], in_=rows)
 
@@ -386,10 +401,10 @@ def tile_list_sounder_bias_features_kernel(
             y_stage[c] = stage_tile([P, width * PACK])
             woven = y_stage[c][:].rearrange("p (c i t) -> p c t i", i=4, t=PACK)
             rows = y_rows[c][:].rearrange("p t (c i) -> p c t i", i=4)
-            if c in WEAVE_ON_VECTOR:
-                nc.vector.tensor_copy(out=woven, in_=rows)
-            else:
+            if c in WEAVE_ON_SCALAR:
                 nc.scalar.copy(out=woven, in_=rows)
+            else:
+                nc.vector.tensor_copy(out=woven, in_=rows)
 
         def quantize_y(c):
             m0, width = CHUNKS[c]
@@ -405,33 +420,33 @@ def tile_list_sounder_bias_features_kernel(
                 in_=tab2_scales[0, 4 * q : 4 * q + 4, :].bitcast(I32).unsqueeze(0).to_broadcast([8, 4, T3 // 4]),
             )
         load_w2(0)
-        nc.sync.dma_start(out=wg2_t[:], in_=wg2)
         load_words(tab_w[0][:], tab_words[0])
         nc.sync.dma_start(lists[0][:], offs)
+        nc.sync.dma_start(out=wg2_t[:], in_=wg2)
         nc.sync.dma_start(lists[3][:], offs4)
         load_w2(1)
-        load_words(tab_w[1][:], tab_words[1])
-        load_planes(tab_s, tab_scales)
-        nc.sync.dma_start(out=w1_w[:].bitcast(I32), in_=w1_words.rearrange("a p c -> p a c").bitcast(I32))
-        load_planes(w1_s, w1_scales)
-        nc.sync.dma_start(out=wg1_t[:], in_=wg1)
-        nc.sync.dma_start(lists[2][:], offs3)
-        nc.sync.dma_start(out=gain_dealt[:], in_=gain[0:KP].rearrange("(p t) -> p t", t=PACK))
         with nc.allow_non_contiguous_dma(reason="one gain for each partition and slice"):
             nc.sync.dma_start(out=gain_rows[:], in_=gain[KP:H].rearrange("(s p) -> p s", p=P))
+        load_planes(tab_s, tab_scales)
+        load_words(tab_w[1][:], tab_words[1])
+        nc.sync.dma_start(out=w1_w[:].bitcast(I32), in_=w1_words.rearrange("a p c -> p a c").bitcast(I32))
+        load_planes(w1_s, w1_scales)
+        load_w2(2)
+        nc.sync.dma_start(out=wg1_t[:], in_=wg1)
+        nc.sync.dma_start(lists[2][:], offs3)
 
         cast_w2(0)
         nc.vector.tensor_copy(v2_w[:], tab2_w[:].indirect(lists[1][:]))
         nc.vector.tensor_copy(v2_s[:], tab2_s[:].indirect(lists[1][:]))
         quantize_w2(0)
         features_b(0)
-        nc.vector.tensor_scalar_mul(wg2_neg[:], wg2_t[:], -1.0)
-        for s in range(4):
-            weigh_b(s)
-        cast_w2(1)
+        load_w3(0)
         load_forecast(0)
-        load_w2(2)
         nc.vector.tensor_copy(v_w[0][:], tab_w[0][:].indirect(lists[0][:]))
+        nc.vector.tensor_scalar_mul(wg2_neg[:], wg2_t[:], -1.0)
+        cast_w2(1)
+        for s in range(SLICES - 1):
+            weigh_b(s)
         nc.gpsimd.memset(pages_a[0][:], 0.0)
         place_b(0)
         quantize_w2(1)
@@ -439,25 +454,28 @@ def tile_list_sounder_bias_features_kernel(
         for a in range(2):
             nc.vector.tensor_copy(v_s[a][:], tab_s[:, T * a : T * (a + 1)].indirect(lists[0][:]))
         features_b(1)
+        for i in (1, 2):
+            nc.gpsimd.memset(pages_a[i][:], 0.0)
         load_forecast(1)
-        load_w3(0)
+        load_w3(1)
         load_forecast(2)
+        nc.sync.dma_start(out=gain_dealt[:], in_=gain[0:KP].rearrange("(p t) -> p t", t=PACK))
         features_a(0)
         place_b(1)
-        nc.gpsimd.memset(pages_a[1][:], 0.0)
         features_a(1)
         cast_w2(2)
-        load_w3(1)
+        cast_w3(0)
+        cast_w3(1)
         place_a(0)
         features_a(2)
         features_b(2)
+        turn_placed(0)
         turn_excess(0)
         load_forecast(3)
-        turn_placed(0)
         place_a(1)
         quantize_w2(2)
-        cast_w3(0)
-        cast_w3(1)
+        features_a(3)
+        features_b(3)
         load_w4()
         turn_excess(1)
         load_forecast(4)
@@ -465,23 +483,23 @@ def tile_list_sounder_bias_features_kernel(
         extras = {
             (2, 0): [lambda: cast_w3(2)],
             (2, 1): [lambda: cast_w3(3)],
-            (3, 0): [lambda: weigh_b(4)],
+            (3, 0): [],
             (3, 1): [],
-            (4, 0): [lambda: weigh_b(5), lambda: z0_part(0, 0), lambda: z0_part(0, 1), lambda: z0_part(0, 2), lambda: z0_part(0, 3)],
+            (4, 0): [lambda: z0_part(0, 0), lambda: z0_part(0, 1), lambda: z0_part(0, 2), lambda: z0_part(0, 3)],
             (4, 1): [],
-            (5, 0): [lambda: weigh_b(6), lambda: z0_part(1, 0), lambda: z0_part(1, 1), lambda: z0_part(1, 2), lambda: z0_part(1, 3)],
+            (5, 0): [lambda: z0_part(1, 0), lambda: z0_part(1, 1), lambda: z0_part(1, 2), lambda: z0_part(1, 3)],
             (5, 1): [],
-            (6, 0): [lambda: weigh_b(7), lambda: z0_weave(0, 0), lambda: z0_weave(0, 1)],
+            (6, 0): [lambda: z0_weave(0, 0), lambda: z0_weave(0, 1)],
             (6, 1): [],
-            (7, 0): [lambda: z0_weave(1, 0), lambda: z0_weave(1, 1)],
+            (7, 0): [lambda: z0_weave(1, 0)],
             (7, 1): [],
         }
         for s in range(2, SLICES):
             last = s == SLICES - 1
             place_a(s)
-            if not last:
-                features_a(s + 1)
-                features_b(s + 1)
+            if s != SLICES - 3 and not last:
+                features_a(min(s + 2, SLICES - 1))
+                features_b(min(s + 2, SLICES - 1))
             if s - 1 < 4:
                 turn_placed(s - 1)
             else:
@@ -489,34 +507,36 @@ def tile_list_sounder_bias_features_kernel(
             for job in extras[(s, 0)]:
                 job()
             if last:
+                quantize_z0(0)
+                weigh_b(s)
+                for c, g in EARLY:
+                    second_pass(c, g, 0)
                 make_peak(s)
+                z0_weave(1, 1)
             place_b(s)
             if s < 4:
                 turn_excess(s)
             elif not last:
                 make_peak(s)
+            if s == SLICES - 2:
+                quantize_w3(0)
             if s + 3 < SLICES:
                 load_forecast(s + 3)
             for job in extras[(s, 1)]:
                 job()
         last = SLICES - 1
-        for pair in range(4):
-            z1_acc[pair] = bank("turned", 3, [P, 2, P]) if pair < 3 else bank("first", 2, [P, 2, P])
-            turn_pair(pair, peak[last], True)
-        for pair in range(4):
-            turn_pair(pair, pages_b[last % 2], False)
-            round_z1(last, pair, z1_acc[pair][:])
+        for g, (b0, n) in enumerate(LAST_BANKS):
+            z1_acc[g] = bank("turned", 3, [P, n, P])
+            turn_blocks(g, peak[last], True)
+        for g, (b0, n) in enumerate(LAST_BANKS):
+            turn_blocks(g, pages_b[last % 2], False)
+            for j in range(0, n, 2):
+                round_z1(last, (b0 + j) // 2, z1_acc[g][:, j : j + 2, :])
 
-        quantize_w3(0)
         quantize_w3(1)
-        quantize_z0(0)
-        make_z1(0)
-        quantize_z1(0)
         deal_w4()
-        make_z1(1)
-        quantize_z1(1)
         quantize_z0(1)
-        for c in range(2, 4):
+        for c in range(4):
             make_z1(c)
             quantize_z1(c)
         for c in range(len(CHUNKS)):

@@ -22,8 +22,8 @@ PACK = 4
 KP = P * PACK
 SLICES = H // P
 BLOCKS = T2 // P
-ROW_PLACES = [0, 8192, 26624]
-Y_PLACES = [4096, 22528, 18432, 26624, 28672]
+ROW_PLACES = [0, 8192, 4096]
+Y_PLACES = [24576, 32768, 28672, 4096, 6144]
 WEAVE_ON_SCALAR = ()
 Z1_ON_VECTOR = ()
 CHUNKS = [(0, 256), (256, 256), (512, 256), (768, 128), (896, 128)]
@@ -90,7 +90,7 @@ def tile_list_sounder_bias_features_kernel(
             tables.tile([P, T], U32, name="tab_w%d" % a, align_bytes=64, offset=4096 + 8192 * a) for a in range(2)
         ]
         tab_s = tables.tile([P, 2 * T], U8, name="tab_s", align_bytes=64, offset=20480)
-        w4_raw_s = tables.tile([P, N], U8, name="w4_raw_s", align_bytes=64, offset=13312)
+        w4_raw_s = held("w4_raw_s", [P, N], U8)
         tab2_s = held("tab2_s", [P, T3], U8)
         v_w = [held("v_w0", [P, S], U32), laid("v_w1", [P, S], U32, 10240)]
         v2_w = held("v2_w", [P, S], U32)
@@ -114,7 +114,7 @@ def tile_list_sounder_bias_features_kernel(
         gain_rows = held("gain_rows", [P, 4], F32)
         ident = held("ident", [P, P], F32)
         pages_a = [
-            tables.tile([P, T2], F32, name="page_a%d" % i, align_bytes=64, offset=(4096, 18432, 22528)[i]) for i in range(3)
+            tables.tile([P, T2], F32, name="page_a%d" % i, align_bytes=64, offset=24576 + 4096 * i) for i in range(3)
         ]
         pages_b = [held("page_b%d" % i, [P, T2], F32) for i in range(2)]
         w2_pieces = [(0, 1), (1, 3), (4, 4)]
@@ -129,11 +129,11 @@ def tile_list_sounder_bias_features_kernel(
         placed = [held("placed%d" % h, [P, 4, PACK, P], F32) for h in range(2)]
         z1_turned = [held("z1_turned%d" % i, [P, 2, 2, P, 2], BF16) for i in range(4)]
 
-        for plane in (tab_s, w1_s):
+        for plane in (tab_s, w1_s, w4_raw_s):
             zero_bytes(nc.vector, plane)
-        nc.vector.memset(pages_b[0][:], 0.0)
+        for page in pages_b + pages_a[0:2]:
+            nc.vector.memset(page[:], 0.0)
         make_identity(nc, ident[:])
-        nc.gpsimd.memset(pages_b[1][:], 0.0)
 
         z1_acc, w4_raw, peak, weight_b, y_acc = {}, {}, {}, {}, {}
         w2_raw, w3_raw, w2_stage, w3_stage, f_rows = {}, {}, {}, {}, {}
@@ -146,7 +146,10 @@ def tile_list_sounder_bias_features_kernel(
 
         def cast_w2(i):
             n = w2_pieces[i][1]
-            w2_stage[i] = stage_tile([P, P * n * PACK])
+            if i == 0:
+                w2_stage[i] = tables.tile([P, P * PACK], BF16, name="first_stage", align_bytes=64, offset=32768)
+            else:
+                w2_stage[i] = stage_tile([P, P * n * PACK])
             nc.scalar.copy(
                 out=w2_stage[i][:].rearrange("p (c i j) -> p c j i", i=4, j=PACK),
                 in_=w2_raw[i][:].rearrange("p j (c i) -> p c j i", i=4),
@@ -178,7 +181,6 @@ def tile_list_sounder_bias_features_kernel(
             nc.sync.dma_start(
                 out=w4_raw["words"][:].bitcast(I32), in_=w4_words.rearrange("a p c i -> p a (c i)").bitcast(I32)
             )
-            zero_bytes(nc.gpsimd, w4_raw_s)
             for q in range(4):
                 nc.sync.dma_start(
                     out=w4_raw_s[32 * q : 32 * q + 8, :].bitcast(I32),
@@ -439,6 +441,7 @@ def tile_list_sounder_bias_features_kernel(
         nc.vector.tensor_copy(v2_w[:], tab2_w[:].indirect(lists[1][:]))
         nc.vector.tensor_copy(v2_s[:], tab2_s[:].indirect(lists[1][:]))
         quantize_w2(0)
+        nc.vector.memset(pages_a[2][:], 0.0)
         features_b(0)
         load_w3(0)
         load_forecast(0)
@@ -447,15 +450,12 @@ def tile_list_sounder_bias_features_kernel(
         cast_w2(1)
         for s in range(SLICES - 1):
             weigh_b(s)
-        nc.gpsimd.memset(pages_a[0][:], 0.0)
         place_b(0)
         quantize_w2(1)
         nc.vector.tensor_copy(v_w[1][:], tab_w[1][:].indirect(lists[0][:]))
         for a in range(2):
             nc.vector.tensor_copy(v_s[a][:], tab_s[:, T * a : T * (a + 1)].indirect(lists[0][:]))
         features_b(1)
-        for i in (1, 2):
-            nc.gpsimd.memset(pages_a[i][:], 0.0)
         load_forecast(1)
         load_w3(1)
         load_forecast(2)

@@ -20,20 +20,47 @@ ALU = mybir.AluOpType
 P = 128
 PACK = 4
 KP = P * PACK
+QUADS = 4
+BANK = 512
+PAIR = 2 * P
+RUN = 4
 SLICES = H // P
-BLOCKS = T2 // P
-ROW_PLACES = [0, 8192, 4096]
-Y_PLACES = [24576, 32768, 28672, 4096, 6144]
-WEAVE_ON_SCALAR = ()
-Z1_ON_VECTOR = ()
+TURNED = SLICES // 2
+LAST = SLICES - 1
+
+W2_PIECES = [(0, 1), (1, 3), (4, 4)]
 CHUNKS = [(0, 256), (256, 256), (512, 256), (768, 128), (896, 128)]
+SCALAR_WEAVES = 2
 EARLY = [(0, 0), (0, 2), (1, 0), (1, 2)]
-LAST_BANKS = [(0, 2), (2, 4), (6, 2)]
-Y_BANKS = [
-    ["first", "back", "first", "turned"], ["back", "turned", "back", "first"], ["first", "turned", "back", "turned"],
-    ["back", "first"], ["back", "first"],
-]
 BANK_BUFS = {"first": 2, "turned": 3, "back": 3}
+Y_BANKS = [
+    ["first", "back", "first", "turned"],
+    ["back", "turned", "back", "first"],
+    ["first", "turned", "back", "turned"],
+    ["back", "first"],
+    ["back", "first"],
+]
+LAST_BANKS = [(0, 2), (2, 4), (6, 2)]
+
+TAB2_WORDS_AT = 0
+TAB_WORDS_AT = [4096, 12288]
+TAB_SCALES_AT = 20480
+V_SCALES_AT = [12288, 12800]
+SECOND_H_B_AT = 13312
+W4_RAW_SCALES_AT = 13312
+PAGE_A_AT = [4096, 18432, 22528]
+ROWS_AT = [0, 8192, 26624]
+Y_ROWS_AT = [4096, 22528, 18432, 26624, 28672]
+
+FIRST_H_B_AT = 10240
+EXCESS_AT = [12288, 20480]
+PEAK_AT = [12288, 20480, 20480, 22528]
+MAX_AT = [28672, 32768, 28672, 2048]
+Z0_WOVEN_AT = [[0, 2048], [28672, 5632]]
+Z0_SCALES_AT = [20480, 512]
+W3_SCALES_AT = [20992, 0]
+LAST_WG2_AT = 0
+W4_SCALES_AT, W4_WORDS_AT = 1024, 1536
 
 
 def tile_list_sounder_bias_features_kernel(
@@ -52,14 +79,11 @@ def tile_list_sounder_bias_features_kernel(
         def held(name, shape, dtype):
             return keep.tile(shape, dtype, name=name, align_bytes=64)
 
-        def laid(name, shape, dtype, offset):
-            return late.tile(shape, dtype, name=name, align_bytes=64, offset=offset)
+        def laid(pool, name, shape, dtype, offset):
+            return pool.tile(shape, dtype, name=name, align_bytes=64, offset=offset)
 
         def stage_tile(shape):
             return work.tile(shape, BF16, name="stage", tag="stage", bufs=6, align_bytes=64)
-
-        def row_tile(i, shape):
-            return tables.tile(shape, F32, name="rows%d" % i, align_bytes=64, offset=ROW_PLACES[i])
 
         def feature_tile():
             return work.tile([P, S], F32, name="feature", tag="feature", bufs=7, align_bytes=64)
@@ -67,92 +91,93 @@ def tile_list_sounder_bias_features_kernel(
         def raw_tile(shape, dtype):
             return work.tile(shape, dtype, name="raw", tag="raw", bufs=3, align_bytes=64)
 
-        def bank(tag, bufs, shape):
-            return psum.tile(shape, F32, name=tag, tag=tag, bufs=bufs)
+        def bank(tag, shape):
+            return psum.tile(shape, F32, name=tag, tag=tag, bufs=BANK_BUFS[tag])
 
         def zero_bytes(engine, tile):
             engine.memset(tile[:].bitcast(I32), 0)
 
-        def load_words(tile_ap, words):
-            nc.sync.dma_start(out=tile_ap.bitcast(I32), in_=words.rearrange("p c i -> p (c i)").bitcast(I32))
+        def load_words(tile, words):
+            nc.sync.dma_start(out=tile[:].bitcast(I32), in_=words.rearrange("p c i -> p (c i)").bitcast(I32))
 
-        def load_planes(tile, scales):
+        def load_scales(tile, scales):
             passes = scales.shape[0]
-            for q in range(4):
+            for q in range(QUADS):
                 nc.sync.dma_start(
                     out=tile[32 * q : 32 * q + 4, :].bitcast(I32).rearrange("r (a w) -> r a w", a=passes),
                     in_=scales[:, 4 * q : 4 * q + 4, :].bitcast(I32).rearrange("a r w -> r a w"),
                 )
 
-        lists = [held("list%d" % i, [P, S // 16], U16) for i in range(4)]
-        tab2_w = tables.tile([P, T3], U32, name="tab2_w", align_bytes=64, offset=0)
-        tab_w = [
-            tables.tile([P, T], U32, name="tab_w%d" % a, align_bytes=64, offset=4096 + 8192 * a) for a in range(2)
-        ]
-        tab_s = tables.tile([P, 2 * T], U8, name="tab_s", align_bytes=64, offset=20480)
-        w4_raw_s = held("w4_raw_s", [P, N], U8)
+        idx, idx2, idx3, idx4 = [held("list%d" % i, [P, S // 16], U16) for i in range(4)]
+        tab2_w = laid(tables, "tab2_w", [P, T3], U32, TAB2_WORDS_AT)
+        tab_w = [laid(tables, "tab_w%d" % a, [P, T], U32, TAB_WORDS_AT[a]) for a in range(2)]
+        tab_s = laid(tables, "tab_s", [P, 2 * T], U8, TAB_SCALES_AT)
+        w4_raw_s = laid(tables, "w4_raw_s", [P, N], U8, W4_RAW_SCALES_AT)
         tab2_s = held("tab2_s", [P, T3], U8)
-        v_w = [held("v_w0", [P, S], U32), laid("v_w1", [P, S], U32, 10240)]
+        v_w = [held("v_w0", [P, S], U32), laid(late, "v_w1", [P, S], U32, FIRST_H_B_AT)]
         v2_w = held("v2_w", [P, S], U32)
         v2_s = held("v2_s", [P, S], U8)
         w1_w = held("w1_w", [P, 2, 2 * H], U8)
         w1_s = held("w1_s", [P, 2 * H], U8)
-        last_wg2 = laid("last_wg2", [P, S], F32, 0)
-        w3_s = [tables.tile([P, N], U8, name="w3_s0", align_bytes=64, offset=0), laid("w3_s1", [P, N], U8, 0)]
-        z0_s = [laid("z0_s0", [P, 512], U8, 20480), laid("z0_s1", [P, 512], U8, 512)]
-        w4_s = laid("w4_s", [P, N], U8, 1024)
-        w4_w = laid("w4_w", [P, 2, N], U32, 1536)
-        first_h_b = laid("first_h_b", [P, S], F32, 10240)
-        v_s = [tables.tile([P, S], U8, name="v_s%d" % a, align_bytes=64, offset=12288 + 512 * a) for a in range(2)]
-        second_h_b = tables.tile([P, S], F32, name="second_h_b", align_bytes=64, offset=13312)
+        last_wg2 = laid(late, "last_wg2", [P, S], F32, LAST_WG2_AT)
+        w3_s = [laid(late, "w3_s%d" % a, [P, N], U8, W3_SCALES_AT[a]) for a in range(2)]
+        z0_s = [laid(late, "z0_s%d" % half, [P, BANK], U8, Z0_SCALES_AT[half]) for half in range(2)]
+        w4_s = laid(late, "w4_s", [P, N], U8, W4_SCALES_AT)
+        w4_w = laid(late, "w4_w", [P, 2, N], U32, W4_WORDS_AT)
+        first_h_b = laid(late, "first_h_b", [P, S], F32, FIRST_H_B_AT)
+        v_s = [laid(tables, "v_s%d" % a, [P, S], U8, V_SCALES_AT[a]) for a in range(2)]
+        second_h_b = laid(tables, "second_h_b", [P, S], F32, SECOND_H_B_AT)
         own_h_b = {0: first_h_b, 1: second_h_b}
         w3_w = [held("w3_w%d" % a, [P, N], U32) for a in range(2)]
         wg1_t = held("wg1_t", [P, S], F32)
         wg2_t = held("wg2_t", [P, S], F32)
         wg2_neg = held("wg2_neg", [P, S], F32)
         gain_dealt = held("gain_dealt", [P, PACK], F32)
-        gain_rows = held("gain_rows", [P, 4], F32)
+        gain_rows = held("gain_rows", [P, SLICES - TURNED], F32)
         ident = held("ident", [P, P], F32)
-        pages_a = [
-            tables.tile([P, T2], F32, name="page_a%d" % i, align_bytes=64, offset=24576 + 4096 * i) for i in range(3)
-        ]
+        pages_a = [laid(tables, "page_a%d" % i, [P, T2], F32, at) for i, at in enumerate(PAGE_A_AT)]
         pages_b = [held("page_b%d" % i, [P, T2], F32) for i in range(2)]
-        w2_pieces = [(0, 1), (1, 3), (4, 4)]
-        w2_w = [held("w2_w%d" % i, [P, P * n], U32) for i, (s0, n) in enumerate(w2_pieces)]
-        w2_s = [held("w2_s%d" % i, [P, P * n], U8) for i, (s0, n) in enumerate(w2_pieces)]
-        z0_w = [held("z0_w%d" % h, [P, 512], U32) for h in range(2)]
-        z1_w = [held("z1_w%d" % pair, [P, 256], U32) for pair in range(4)]
-        z1_s = [held("z1_s%d" % pair, [P, 256], U8) for pair in range(4)]
+        w2_w = [held("w2_w%d" % i, [P, P * n], U32) for i, (s0, n) in enumerate(W2_PIECES)]
+        w2_s = [held("w2_s%d" % i, [P, P * n], U8) for i, (s0, n) in enumerate(W2_PIECES)]
+        z0_w = [held("z0_w%d" % half, [P, BANK], U32) for half in range(2)]
+        z1_w = [held("z1_w%d" % pair, [P, PAIR], U32) for pair in range(T2 // PAIR)]
+        z1_s = [held("z1_s%d" % pair, [P, PAIR], U8) for pair in range(T2 // PAIR)]
         y_w = [held("y_w%d" % c, [P, width], U32) for c, (m0, width) in enumerate(CHUNKS)]
         y_s = held("y_s", [P, T2], U8)
-        excess = [laid("excess%d" % h, [P, 4, PACK, P], F32, 12288 + 8192 * h) for h in range(2)]
-        placed = [held("placed%d" % h, [P, 4, PACK, P], F32) for h in range(2)]
-        z1_turned = [held("z1_turned%d" % i, [P, 2, 2, P, 2], BF16) for i in range(4)]
+        excess = [laid(late, "excess%d" % half, [P, 4, PACK, P], F32, EXCESS_AT[half]) for half in range(2)]
+        placed = [held("placed%d" % half, [P, 4, PACK, P], F32) for half in range(2)]
+        z1_turned = [held("z1_turned%d" % pair, [P, 2, 2, P, 2], BF16) for pair in range(T2 // PAIR)]
 
-        for plane in (tab_s, w1_s, w4_raw_s):
-            zero_bytes(nc.vector, plane)
-        for page in pages_b + pages_a[0:2]:
-            nc.vector.memset(page[:], 0.0)
+        for scale_tile in (tab_s, w1_s):
+            zero_bytes(nc.vector, scale_tile)
+        nc.vector.memset(pages_b[0][:], 0.0)
         make_identity(nc, ident[:])
+        nc.gpsimd.memset(pages_b[1][:], 0.0)
 
         z1_acc, w4_raw, peak, weight_b, y_acc = {}, {}, {}, {}, {}
         w2_raw, w3_raw, w2_stage, w3_stage, f_rows = {}, {}, {}, {}, {}
-        h_a, h_b, z0_rows, z0_stage, z1_stage, y_rows, y_stage = {}, {}, {}, {}, {}, {}, {}
+        h_a, h_b, z0_rows, z0_woven, z1_woven, y_rows, y_woven = {}, {}, {}, {}, {}, {}, {}
+
+        def page_a(s):
+            return pages_a[s % len(pages_a)]
+
+        def page_b(s):
+            return pages_b[s % len(pages_b)]
+
+        def row_gain(s):
+            return gain_rows[:, s - TURNED : s - TURNED + 1]
 
         def load_w2(i):
-            s0, n = w2_pieces[i]
+            s0, n = W2_PIECES[i]
             w2_raw[i] = raw_tile([P, PACK, P * n], F32)
             nc.sync.dma_start(out=w2_raw[i][:], in_=w2[:, P * s0 : P * (s0 + n)].rearrange("(p j) c -> p j c", j=PACK))
 
         def cast_w2(i):
-            n = w2_pieces[i][1]
-            if i == 0:
-                w2_stage[i] = tables.tile([P, P * PACK], BF16, name="first_stage", align_bytes=64, offset=32768)
-            else:
-                w2_stage[i] = stage_tile([P, P * n * PACK])
+            n = W2_PIECES[i][1]
+            w2_stage[i] = stage_tile([P, P * n * PACK])
             nc.scalar.copy(
-                out=w2_stage[i][:].rearrange("p (c i j) -> p c j i", i=4, j=PACK),
-                in_=w2_raw[i][:].rearrange("p j (c i) -> p c j i", i=4),
+                out=w2_stage[i][:].rearrange("p (c i j) -> p c j i", i=RUN, j=PACK),
+                in_=w2_raw[i][:].rearrange("p j (c i) -> p c j i", i=RUN),
             )
 
         def quantize_w2(i):
@@ -162,13 +187,13 @@ def tile_list_sounder_bias_features_kernel(
             w3_raw[a] = raw_tile([P, PACK, N], F32)
             nc.sync.dma_start(out=w3_raw[a][:], in_=w3[KP * a : KP * (a + 1), :].rearrange("(p j) c -> p j c", j=PACK))
 
-        def cast_w3(i):
-            a, half = divmod(i, 2)
+        def cast_w3(a, half):
             if half == 0:
                 w3_stage[a] = stage_tile([P, PACK, P, PACK])
+            quads, cols = P // 2, N // 2
             nc.scalar.copy(
-                out=w3_stage[a][:, :, 64 * half : 64 * (half + 1), :].rearrange("p t q j -> p q j t"),
-                in_=w3_raw[a][:, :, 256 * half : 256 * (half + 1)].rearrange("p j (q t) -> p q j t", t=PACK),
+                out=w3_stage[a][:, :, quads * half : quads * (half + 1), :].rearrange("p t q j -> p q j t"),
+                in_=w3_raw[a][:, :, cols * half : cols * (half + 1)].rearrange("p j (q t) -> p q j t", t=PACK),
             )
 
         def quantize_w3(a):
@@ -181,7 +206,8 @@ def tile_list_sounder_bias_features_kernel(
             nc.sync.dma_start(
                 out=w4_raw["words"][:].bitcast(I32), in_=w4_words.rearrange("a p c i -> p a (c i)").bitcast(I32)
             )
-            for q in range(4):
+            zero_bytes(nc.gpsimd, w4_raw_s)
+            for q in range(QUADS):
                 nc.sync.dma_start(
                     out=w4_raw_s[32 * q : 32 * q + 8, :].bitcast(I32),
                     in_=w4_scales[:, 4 * q : 4 * q + 4, :].bitcast(I32),
@@ -189,8 +215,8 @@ def tile_list_sounder_bias_features_kernel(
 
         def deal_w4():
             nc.vector.tensor_copy(
-                out=w4_w[:].bitcast(I32).rearrange("p a (t c i) -> p a c t i", t=PACK, i=4),
-                in_=w4_raw["words"][:].bitcast(I32).rearrange("p a (c i t) -> p a c t i", t=PACK, i=4),
+                out=w4_w[:].bitcast(I32).rearrange("p a (t c i) -> p a c t i", t=PACK, i=RUN),
+                in_=w4_raw["words"][:].bitcast(I32).rearrange("p a (c i t) -> p a c t i", t=PACK, i=RUN),
             )
             nc.vector.tensor_copy(
                 out=w4_s[:].rearrange("p (t q) -> p q t", t=PACK),
@@ -198,11 +224,12 @@ def tile_list_sounder_bias_features_kernel(
             )
 
         def load_forecast(s):
-            f_rows[s] = row_tile(s % 3, [P, T2])
+            place = s % len(ROWS_AT)
+            f_rows[s] = laid(tables, "rows%d" % place, [P, T2], F32, ROWS_AT[place])
             nc.sync.dma_start(out=f_rows[s][:], in_=forecast[P * s : P * (s + 1), :])
 
         def features_a(s):
-            acc = bank("first", 2, [P, S])
+            acc = bank("first", [P, S])
             for a in range(2):
                 nc.tensor.matmul_mx(
                     out=acc[:],
@@ -214,12 +241,12 @@ def tile_list_sounder_bias_features_kernel(
                     stop=(a == 1),
                 )
             h_a[s] = feature_tile()
-            nc.scalar.activation(out=h_a[s][:], in_=acc[:], func=ACT.Tanh, scale=(-1.0 if s < 4 else 1.0))
+            nc.scalar.activation(out=h_a[s][:], in_=acc[:], func=ACT.Tanh, scale=(-1.0 if s < TURNED else 1.0))
 
         def features_b(s):
-            i = max(j for j, (s0, n) in enumerate(w2_pieces) if s0 <= s)
-            cols = slice(P * (s - w2_pieces[i][0]), P * (s - w2_pieces[i][0] + 1))
-            acc = bank("first", 2, [P, S])
+            i = max(j for j, (s0, n) in enumerate(W2_PIECES) if s0 <= s)
+            cols = slice(P * (s - W2_PIECES[i][0]), P * (s - W2_PIECES[i][0] + 1))
+            acc = bank("first", [P, S])
             nc.tensor.matmul_mx(
                 out=acc[:],
                 lhsT=w2_w[i][:, cols].bitcast(FP8X4),
@@ -234,17 +261,15 @@ def tile_list_sounder_bias_features_kernel(
 
         def weigh_b(s):
             weight_b[s] = wg2_neg
-            if s >= 4:
-                weight_b[s] = last_wg2 if s == SLICES - 1 else held("wg2_gain%d" % s, [P, S], F32)
-                nc.scalar.activation(
-                    out=weight_b[s][:], in_=wg2_t[:], func=ACT.Copy, scale=gain_rows[:, s - 4 : s - 3]
-                )
+            if s >= TURNED:
+                weight_b[s] = last_wg2 if s == LAST else held("wg2_gain%d" % s, [P, S], F32)
+                nc.scalar.activation(out=weight_b[s][:], in_=wg2_t[:], func=ACT.Copy, scale=row_gain(s))
 
         def place_a(s):
-            nc.vector.tensor_tensor(pages_a[s % 3][:].indirect(lists[2][:]), h_a[s][:], wg1_t[:], ALU.mult)
+            nc.vector.tensor_tensor(page_a(s)[:].indirect(idx3[:]), h_a[s][:], wg1_t[:], ALU.mult)
 
         def place_b(s):
-            nc.vector.tensor_tensor(pages_b[s % 2][:].indirect(lists[3][:]), h_b[s][:], weight_b[s][:], ALU.mult)
+            nc.vector.tensor_tensor(page_b(s)[:].indirect(idx4[:]), h_b[s][:], weight_b[s][:], ALU.mult)
 
         def add_turned(out, first, second):
             nc.tensor.matmul(out, lhsT=first, rhs=ident[:], start=True, stop=False, is_transpose=True)
@@ -253,11 +278,15 @@ def tile_list_sounder_bias_features_kernel(
         def block_of(tile, b):
             return tile[:, P * b : P * (b + 1)]
 
+        def turned_half(half, first, second):
+            acc = bank("turned", [P, 4, P])
+            for b in range(4):
+                add_turned(acc[:, b, :], block_of(first, 4 * half + b), block_of(second, 4 * half + b))
+            return acc
+
         def turn_sum(s, first, second, dest, func, scale):
             for half in range(2):
-                acc = bank("turned", 3, [P, 4, P])
-                for b in range(4):
-                    add_turned(acc[:, b, :], block_of(first, 4 * half + b), block_of(second, 4 * half + b))
+                acc = turned_half(half, first, second)
                 nc.scalar.activation(
                     out=dest[half][:, :, :, 32 * s : 32 * (s + 1)],
                     in_=acc[:].rearrange("m b (p t) -> m b t p", t=PACK),
@@ -266,19 +295,48 @@ def tile_list_sounder_bias_features_kernel(
                 )
 
         def turn_excess(s):
-            turn_sum(s, f_rows[s], pages_a[s % 3], excess, ACT.Relu, 1.0)
+            turn_sum(s, f_rows[s], page_a(s), excess, ACT.Relu, 1.0)
 
         def turn_placed(s):
-            turn_sum(s, pages_a[s % 3], pages_b[s % 2], placed, ACT.Copy, -1.0)
+            turn_sum(s, page_a(s), page_b(s), placed, ACT.Copy, -1.0)
+
+        def z0_back(half):
+            z0_rows[half] = stage_tile([P, PACK, BANK])
+            for t in range(PACK):
+                acc = bank("back", [P, 4, P])
+                for b in range(4):
+                    add_turned(acc[:, b, :], excess[half][:, b, t, :], placed[half][:, b, t, :])
+                nc.scalar.activation(
+                    out=z0_rows[half][:, t, :],
+                    in_=acc[:].rearrange("p b m -> p (b m)"),
+                    func=ACT.Copy,
+                    scale=gain_dealt[:, t : t + 1],
+                )
+
+        def z0_weave(half, part):
+            z0_woven[half, part] = laid(
+                late, "z0_woven%d%d" % (half, part), [P, PAIR * PACK], BF16, Z0_WOVEN_AT[half][part]
+            )
+            nc.scalar.copy(
+                out=z0_woven[half, part][:].rearrange("p (c i t) -> p c t i", i=RUN, t=PACK),
+                in_=z0_rows[half][:, :, PAIR * part : PAIR * (part + 1)].rearrange("p t (c i) -> p c t i", i=RUN),
+            )
+
+        def quantize_z0(half):
+            for part in range(2):
+                cols = slice(PAIR * part, PAIR * (part + 1))
+                nc.vector.quantize_mx(
+                    out=z0_w[half][:, cols].bitcast(FP8X4), scales=z0_s[half][:, cols], in_=z0_woven[half, part][:]
+                )
 
         def make_peak(s):
-            plain = laid("plain_peak%d" % s, [P, T2], F32, (28672, 32768, 28672, 2048)[s - 4])
-            nc.vector.tensor_tensor(plain[:], pages_a[s % 3][:], f_rows[s][:], ALU.max)
-            peak[s] = laid("peak%d" % s, [P, T2], F32, (12288, 20480, 20480, 22528)[s - 4])
-            nc.scalar.activation(out=peak[s][:], in_=plain[:], func=ACT.Copy, scale=gain_rows[:, s - 4 : s - 3])
+            larger = laid(late, "larger%d" % s, [P, T2], F32, MAX_AT[s - TURNED])
+            nc.vector.tensor_tensor(larger[:], page_a(s)[:], f_rows[s][:], ALU.max)
+            peak[s] = laid(late, "peak%d" % s, [P, T2], F32, PEAK_AT[s - TURNED])
+            nc.scalar.activation(out=peak[s][:], in_=larger[:], func=ACT.Copy, scale=row_gain(s))
 
         def round_z1(s, pair, acc):
-            quarter = s - 4
+            quarter = s - TURNED
             nc.scalar.copy(
                 out=z1_turned[pair][:, :, :, 32 * quarter : 32 * (quarter + 1), :],
                 in_=acc.rearrange("m b (p u e) -> m b u p e", u=2, e=2),
@@ -286,13 +344,11 @@ def tile_list_sounder_bias_features_kernel(
 
         def turn_z1(s):
             for half in range(2):
-                acc = bank("turned", 3, [P, 4, P])
-                for b in range(4):
-                    add_turned(acc[:, b, :], block_of(peak[s], 4 * half + b), block_of(pages_b[s % 2], 4 * half + b))
+                acc = turned_half(half, peak[s], page_b(s))
                 for j in range(2):
                     round_z1(s, 2 * half + j, acc[:, 2 * j : 2 * j + 2, :])
 
-        def turn_blocks(g, source, opens):
+        def turn_last(g, source, opens):
             b0, n = LAST_BANKS[g]
             for j in range(n):
                 nc.tensor.matmul(
@@ -304,70 +360,39 @@ def tile_list_sounder_bias_features_kernel(
                     is_transpose=True,
                 )
 
-        def z0_part(half, t):
-            if t == 0:
-                z0_rows[half] = stage_tile([P, PACK, 512])
-            acc = bank("back", 3, [P, 4, P])
-            for b in range(4):
-                add_turned(acc[:, b, :], excess[half][:, b, t, :], placed[half][:, b, t, :])
-            nc.scalar.activation(
-                out=z0_rows[half][:, t, :],
-                in_=acc[:].rearrange("p b m -> p (b m)"),
-                func=ACT.Copy,
-                scale=gain_dealt[:, t : t + 1],
-            )
-
-        def z0_weave(half, part):
-            z0_stage[half, part] = laid(
-                "z0_stage%d%d" % (half, part), [P, 256 * PACK], BF16, ((0, 2048), (28672, 5632))[half][part]
-            )
-            nc.scalar.copy(
-                out=z0_stage[half, part][:].rearrange("p (c i t) -> p c t i", i=4, t=PACK),
-                in_=z0_rows[half][:, :, 256 * part : 256 * (part + 1)].rearrange("p t (c i) -> p c t i", i=4),
-            )
-
-        def quantize_z0(half):
-            for part in range(2):
-                cols = slice(256 * part, 256 * (part + 1))
-                nc.vector.quantize_mx(
-                    out=z0_w[half][:, cols].bitcast(FP8X4), scales=z0_s[half][:, cols], in_=z0_stage[half, part][:]
-                )
-
-        def make_z1(c):
-            z1_stage[c] = stage_tile([P, 256 * PACK])
-            acc = bank("turned", 3, [P, 2, 2, P])
+        def weave_z1(pair):
+            z1_woven[pair] = stage_tile([P, PAIR * PACK])
+            acc = bank("turned", [P, 2, 2, P])
             for b in range(2):
                 for u in range(2):
-                    words = z1_turned[c][:, b, u, :, :].rearrange("m p e -> m (p e)").bitcast(F32)
+                    words = z1_turned[pair][:, b, u, :, :].rearrange("m p e -> m (p e)").bitcast(F32)
                     nc.tensor.transpose(acc[:, b, u, :], words, ident[:])
-            woven = z1_stage[c][:].bitcast(F32).rearrange("p (b m u) -> p b m u", b=2, u=2)
-            if c in Z1_ON_VECTOR:
-                nc.vector.tensor_copy(out=woven, in_=acc[:].rearrange("p b u m -> p b m u"))
-            else:
-                nc.scalar.copy(out=woven, in_=acc[:].rearrange("p b u m -> p b m u"))
+            nc.scalar.copy(
+                out=z1_woven[pair][:].bitcast(F32).rearrange("p (b m u) -> p b m u", b=2, u=2),
+                in_=acc[:].rearrange("p b u m -> p b m u"),
+            )
 
-        def quantize_z1(c):
-            nc.vector.quantize_mx(out=z1_w[c][:].bitcast(FP8X4), scales=z1_s[c][:], in_=z1_stage[c][:])
+        def quantize_z1(pair):
+            nc.vector.quantize_mx(out=z1_w[pair][:].bitcast(FP8X4), scales=z1_s[pair][:], in_=z1_woven[pair][:])
 
         def second_pass(c, g, a):
             m0, width = CHUNKS[c]
-            share = 512 // width
+            share = BANK // width
             t0 = share * (g // 2)
             if a == 0:
-                tag = Y_BANKS[c][g]
-                y_acc[c, g] = bank(tag, BANK_BUFS[tag], [P, share, width])
-                half, first = divmod(m0, 512)
+                y_acc[c, g] = bank(Y_BANKS[c][g], [P, share, width])
+                half, first = divmod(m0, BANK)
                 words, scales = z0_w[half], z0_s[half]
             else:
-                pair, first = divmod(m0, 256)
+                pair, first = divmod(m0, PAIR)
                 words, scales = z1_w[pair], z1_s[pair]
             cols = slice(first, first + width)
             for j in range(share):
-                rows = slice(P * (t0 + j), P * (t0 + j + 1))
+                dealt = slice(P * (t0 + j), P * (t0 + j + 1))
                 nc.tensor.matmul_mx(
                     out=y_acc[c, g][:, j, :],
-                    lhsT=(w4_w[:, a, rows] if g % 2 else w3_w[a][:, rows]).bitcast(FP8X4),
-                    lhsT_scale=w4_s[4 * a : P, rows] if g % 2 else w3_s[a][:, rows],
+                    lhsT=(w4_w[:, a, dealt] if g % 2 else w3_w[a][:, dealt]).bitcast(FP8X4),
+                    lhsT_scale=w4_s[4 * a : P, dealt] if g % 2 else w3_s[a][:, dealt],
                     rhs=words[:, cols].bitcast(FP8X4),
                     rhs_scale=scales[:, cols],
                     start=(a == 0 and j == 0),
@@ -384,9 +409,9 @@ def tile_list_sounder_bias_features_kernel(
 
         def make_y(c):
             m0, width = CHUNKS[c]
-            share = 512 // width
-            y_rows[c] = tables.tile([P, PACK, width], F32, name="y_rows%d" % c, align_bytes=64, offset=Y_PLACES[c])
-            for g in range(0, 2 * PACK // share, 2):
+            share = BANK // width
+            y_rows[c] = laid(tables, "y_rows%d" % c, [P, PACK, width], F32, Y_ROWS_AT[c])
+            for g in range(0, len(Y_BANKS[c]), 2):
                 t0 = share * (g // 2)
                 finish_sum(c, g)
                 bent = feature_tile()
@@ -400,72 +425,77 @@ def tile_list_sounder_bias_features_kernel(
 
         def weave_y(c):
             width = CHUNKS[c][1]
-            y_stage[c] = stage_tile([P, width * PACK])
-            woven = y_stage[c][:].rearrange("p (c i t) -> p c t i", i=4, t=PACK)
-            rows = y_rows[c][:].rearrange("p t (c i) -> p c t i", i=4)
-            if c in WEAVE_ON_SCALAR:
-                nc.scalar.copy(out=woven, in_=rows)
+            y_woven[c] = stage_tile([P, width * PACK])
+            woven = y_woven[c][:].rearrange("p (c i t) -> p c t i", i=RUN, t=PACK)
+            rows = y_rows[c][:].rearrange("p t (c i) -> p c t i", i=RUN)
+            if c < SCALAR_WEAVES:
+                runs = P // RUN
+                for first in range(0, width // RUN, runs):
+                    nc.scalar.copy(out=woven[:, first : first + runs], in_=rows[:, first : first + runs])
             else:
                 nc.vector.tensor_copy(out=woven, in_=rows)
 
         def quantize_y(c):
             m0, width = CHUNKS[c]
             cols = slice(m0, m0 + width)
-            nc.vector.quantize_mx(out=y_w[c][:].bitcast(FP8X4), scales=y_s[:, cols], in_=y_stage[c][:])
+            nc.vector.quantize_mx(out=y_w[c][:].bitcast(FP8X4), scales=y_s[:, cols], in_=y_woven[c][:])
             nc.sync.dma_start(out=out_words[:, cols], in_=y_w[c][:].bitcast(I32))
 
-        nc.sync.dma_start(lists[1][:], offs2)
-        load_words(tab2_w[:], tab2_words[0])
-        for q in range(4):
+        nc.sync.dma_start(idx2[:], offs2)
+        load_words(tab2_w, tab2_words[0])
+        for q in range(QUADS):
             nc.sync.dma_start(
                 out=tab2_s[32 * q : 32 * (q + 1), :].bitcast(I32),
                 in_=tab2_scales[0, 4 * q : 4 * q + 4, :].bitcast(I32).unsqueeze(0).to_broadcast([8, 4, T3 // 4]),
             )
         load_w2(0)
-        load_words(tab_w[0][:], tab_words[0])
-        nc.sync.dma_start(lists[0][:], offs)
+        load_words(tab_w[0], tab_words[0])
+        nc.sync.dma_start(idx[:], offs)
         nc.sync.dma_start(out=wg2_t[:], in_=wg2)
-        nc.sync.dma_start(lists[3][:], offs4)
+        nc.sync.dma_start(idx4[:], offs4)
         load_w2(1)
         with nc.allow_non_contiguous_dma(reason="one gain for each partition and slice"):
             nc.sync.dma_start(out=gain_rows[:], in_=gain[KP:H].rearrange("(s p) -> p s", p=P))
-        load_planes(tab_s, tab_scales)
-        load_words(tab_w[1][:], tab_words[1])
+        load_scales(tab_s, tab_scales)
+        load_words(tab_w[1], tab_words[1])
         nc.sync.dma_start(out=w1_w[:].bitcast(I32), in_=w1_words.rearrange("a p c -> p a c").bitcast(I32))
-        load_planes(w1_s, w1_scales)
+        load_scales(w1_s, w1_scales)
         load_w2(2)
         nc.sync.dma_start(out=wg1_t[:], in_=wg1)
-        nc.sync.dma_start(lists[2][:], offs3)
+        nc.sync.dma_start(idx3[:], offs3)
 
         cast_w2(0)
-        nc.vector.tensor_copy(v2_w[:], tab2_w[:].indirect(lists[1][:]))
-        nc.vector.tensor_copy(v2_s[:], tab2_s[:].indirect(lists[1][:]))
+        nc.vector.tensor_copy(v2_w[:], tab2_w[:].indirect(idx2[:]))
+        nc.vector.tensor_copy(v2_s[:], tab2_s[:].indirect(idx2[:]))
         quantize_w2(0)
-        nc.vector.memset(pages_a[2][:], 0.0)
         features_b(0)
         load_w3(0)
         load_forecast(0)
-        nc.vector.tensor_copy(v_w[0][:], tab_w[0][:].indirect(lists[0][:]))
+        nc.vector.tensor_copy(v_w[0][:], tab_w[0][:].indirect(idx[:]))
         nc.vector.tensor_scalar_mul(wg2_neg[:], wg2_t[:], -1.0)
         cast_w2(1)
-        for s in range(SLICES - 1):
+        for s in range(LAST):
             weigh_b(s)
+        nc.gpsimd.memset(pages_a[0][:], 0.0)
         place_b(0)
         quantize_w2(1)
-        nc.vector.tensor_copy(v_w[1][:], tab_w[1][:].indirect(lists[0][:]))
+        nc.vector.tensor_copy(v_w[1][:], tab_w[1][:].indirect(idx[:]))
         for a in range(2):
-            nc.vector.tensor_copy(v_s[a][:], tab_s[:, T * a : T * (a + 1)].indirect(lists[0][:]))
+            nc.vector.tensor_copy(v_s[a][:], tab_s[:, T * a : T * (a + 1)].indirect(idx[:]))
         features_b(1)
+        for page in pages_a[1:]:
+            nc.gpsimd.memset(page[:], 0.0)
         load_forecast(1)
         load_w3(1)
         load_forecast(2)
         nc.sync.dma_start(out=gain_dealt[:], in_=gain[0:KP].rearrange("(p t) -> p t", t=PACK))
+
         features_a(0)
         place_b(1)
         features_a(1)
         cast_w2(2)
-        cast_w3(0)
-        cast_w3(1)
+        cast_w3(0, 0)
+        cast_w3(0, 1)
         place_a(0)
         features_a(2)
         features_b(2)
@@ -480,72 +510,63 @@ def tile_list_sounder_bias_features_kernel(
         turn_excess(1)
         load_forecast(4)
 
-        extras = {
-            (2, 0): [lambda: cast_w3(2)],
-            (2, 1): [lambda: cast_w3(3)],
-            (3, 0): [],
-            (3, 1): [],
-            (4, 0): [lambda: z0_part(0, 0), lambda: z0_part(0, 1), lambda: z0_part(0, 2), lambda: z0_part(0, 3)],
-            (4, 1): [],
-            (5, 0): [lambda: z0_part(1, 0), lambda: z0_part(1, 1), lambda: z0_part(1, 2), lambda: z0_part(1, 3)],
-            (5, 1): [],
-            (6, 0): [lambda: z0_weave(0, 0), lambda: z0_weave(0, 1)],
-            (6, 1): [],
-            (7, 0): [lambda: z0_weave(1, 0)],
-            (7, 1): [],
-        }
         for s in range(2, SLICES):
-            last = s == SLICES - 1
             place_a(s)
-            if s != SLICES - 3 and not last:
-                features_a(min(s + 2, SLICES - 1))
-                features_b(min(s + 2, SLICES - 1))
-            if s - 1 < 4:
+            ahead = {LAST - 2: None, LAST - 1: LAST, LAST: None}.get(s, s + 2)
+            if ahead is not None:
+                features_a(ahead)
+                features_b(ahead)
+            if s - 1 < TURNED:
                 turn_placed(s - 1)
             else:
                 turn_z1(s - 1)
-            for job in extras[(s, 0)]:
-                job()
-            if last:
+            if s == 2:
+                cast_w3(1, 0)
+            if s in (TURNED, TURNED + 1):
+                z0_back(s - TURNED)
+            if s == LAST - 1:
+                z0_weave(0, 0)
+                z0_weave(0, 1)
+            if s == LAST:
+                z0_weave(1, 0)
                 quantize_z0(0)
+                quantize_w3(0)
                 weigh_b(s)
                 for c, g in EARLY:
                     second_pass(c, g, 0)
                 make_peak(s)
                 z0_weave(1, 1)
             place_b(s)
-            if s < 4:
+            if s < TURNED:
                 turn_excess(s)
-            elif not last:
+            elif s < LAST:
                 make_peak(s)
-            if s == SLICES - 2:
-                quantize_w3(0)
-            if s + 3 < SLICES:
-                load_forecast(s + 3)
-            for job in extras[(s, 1)]:
-                job()
-        last = SLICES - 1
+            if s + len(ROWS_AT) < SLICES:
+                load_forecast(s + len(ROWS_AT))
+            if s == 2:
+                cast_w3(1, 1)
+
         for g, (b0, n) in enumerate(LAST_BANKS):
-            z1_acc[g] = bank("turned", 3, [P, n, P])
-            turn_blocks(g, peak[last], True)
+            z1_acc[g] = bank("turned", [P, n, P])
+            turn_last(g, peak[LAST], True)
         for g, (b0, n) in enumerate(LAST_BANKS):
-            turn_blocks(g, pages_b[last % 2], False)
+            turn_last(g, page_b(LAST), False)
             for j in range(0, n, 2):
-                round_z1(last, (b0 + j) // 2, z1_acc[g][:, j : j + 2, :])
+                round_z1(LAST, (b0 + j) // 2, z1_acc[g][:, j : j + 2, :])
 
         quantize_w3(1)
         deal_w4()
         quantize_z0(1)
-        for c in range(4):
-            make_z1(c)
-            quantize_z1(c)
+        for pair in range(T2 // PAIR):
+            weave_z1(pair)
+            quantize_z1(pair)
         for c in range(len(CHUNKS)):
             make_y(c)
             if c > 0:
                 quantize_y(c - 1)
             weave_y(c)
         quantize_y(len(CHUNKS) - 1)
-        for q in range(4):
+        for q in range(QUADS):
             nc.sync.dma_start(
                 out=out_2[0, 4 * q : 4 * q + 4, :].bitcast(I32), in_=y_s[32 * q : 32 * q + 4, :].bitcast(I32)
             )

from contextlib import ExitStack

import concourse.mybir as mybir
from concourse.masks import make_identity

K, K2, H, N, T, T3, S, T2 = 1024, 512, 1024, 512, 2048, 1024, 512, 1024
FLOPS = 2 * S * H * (K + K2) + 2 * 2 * H * N * T2

F32 = mybir.dt.float32
BF16 = mybir.dt.bfloat16
I32 = mybir.dt.int32
U32 = mybir.dt.uint32
U16 = mybir.dt.uint16
U8 = mybir.dt.uint8
FP8X4 = mybir.dt.float8_e4m3fn_x4
FP4X4 = mybir.dt.float4_e2m1fn_x4
ACT = mybir.ActivationFunctionType
ALU = mybir.AluOpType

P = 128
PACK = 4
KP = P * PACK
QUADS = 4
BANK = 512
PAIR = 2 * P
RUN = 4
SLICES = H // P
TURNED = SLICES // 2
LAST = SLICES - 1

W2_PIECES = [(0, 1), (1, 3), (4, 4)]
CHUNKS = [(0, 256), (256, 256), (512, 256), (768, 128), (896, 128)]
SCALAR_WEAVES = 2
EARLY = [(0, 0), (0, 2), (1, 0), (1, 2)]
BANK_BUFS = {"first": 2, "turned": 3, "back": 3}
Y_BANKS = [
    ["first", "back", "first", "turned"],
    ["back", "turned", "back", "first"],
    ["first", "turned", "back", "turned"],
    ["back", "first"],
    ["back", "first"],
]
LAST_BANKS = [(0, 2), (2, 4), (6, 2)]

TAB2_WORDS_AT = 0
TAB_WORDS_AT = [4096, 12288]
TAB_SCALES_AT = 20480
V_SCALES_AT = [12288, 12800]
SECOND_H_B_AT = 13312
W4_RAW_SCALES_AT = 13312
PAGE_A_AT = [4096, 18432, 22528]
ROWS_AT = [0, 8192, 26624]
Y_ROWS_AT = [4096, 22528, 18432, 26624, 28672]

FIRST_H_B_AT = 10240
EXCESS_AT = [12288, 20480]
PEAK_AT = [12288, 20480, 20480, 22528]
MAX_AT = [28672, 32768, 28672, 2048]
Z0_WOVEN_AT = [[0, 2048], [28672, 5632]]
Z0_SCALES_AT = [20480, 512]
W3_SCALES_AT = [20992, 0]
LAST_WG2_AT = 0
W4_SCALES_AT, W4_WORDS_AT = 1024, 1536


def tile_list_sounder_bias_features_kernel(
    tc, tab_words, tab_scales, tab2_words, tab2_scales, offs, offs2, offs3, offs4,
    w1_words, w1_scales, w2, w3, w4_words, w4_scales, forecast, gain, wg1, wg2,
    out_0, out_1, out_2,
):
    nc = tc.nc
    with ExitStack() as ctx:
        keep = ctx.enter_context(tc.tile_pool(name="keep", bufs=1))
        late = ctx.enter_context(tc.tile_pool(name="late", bufs=1))
        tables = ctx.enter_context(tc.tile_pool(name="tables", bufs=1))
        work = ctx.enter_context(tc.tile_pool(name="work", bufs=2))
        psum = ctx.enter_context(tc.psum_pool(name="psum", bufs=2))

        def held(name, shape, dtype):
            return keep.tile(shape, dtype, name=name, align_bytes=64)

        def laid(pool, name, shape, dtype, offset):
            return pool.tile(shape, dtype, name=name, align_bytes=64, offset=offset)

        def stage_tile(shape):
            return work.tile(shape, BF16, name="stage", tag="stage", bufs=6, align_bytes=64)

        def feature_tile():
            return work.tile([P, S], F32, name="feature", tag="feature", bufs=7, align_bytes=64)

        def raw_tile(shape, dtype):
            return work.tile(shape, dtype, name="raw", tag="raw", bufs=3, align_bytes=64)

        def bank(tag, shape):
            return psum.tile(shape, F32, name=tag, tag=tag, bufs=BANK_BUFS[tag])

        def zero_bytes(engine, tile):
            engine.memset(tile[:].bitcast(I32), 0)

        def load_words(tile, words):
            nc.sync.dma_start(out=tile[:].bitcast(I32), in_=words.rearrange("p c i -> p (c i)").bitcast(I32))

        def load_scales(tile, scales):
            passes = scales.shape[0]
            for q in range(QUADS):
                nc.sync.dma_start(
                    out=tile[32 * q : 32 * q + 4, :].bitcast(I32).rearrange("r (a w) -> r a w", a=passes),
                    in_=scales[:, 4 * q : 4 * q + 4, :].bitcast(I32).rearrange("a r w -> r a w"),
                )

        idx, idx2, idx3, idx4 = [held("list%d" % i, [P, S // 16], U16) for i in range(4)]
        tab2_w = laid(tables, "tab2_w", [P, T3], U32, TAB2_WORDS_AT)
        tab_w = [laid(tables, "tab_w%d" % a, [P, T], U32, TAB_WORDS_AT[a]) for a in range(2)]
        tab_s = laid(tables, "tab_s", [P, 2 * T], U8, TAB_SCALES_AT)
        w4_raw_s = laid(tables, "w4_raw_s", [P, N], U8, W4_RAW_SCALES_AT)
        tab2_s = held("tab2_s", [P, T3], U8)
        v_w = [held("v_w0", [P, S], U32), laid(late, "v_w1", [P, S], U32, FIRST_H_B_AT)]
        v2_w = held("v2_w", [P, S], U32)
        v2_s = held("v2_s", [P, S], U8)
        w1_w = held("w1_w", [P, 2, 2 * H], U8)
        w1_s = held("w1_s", [P, 2 * H], U8)
        last_wg2 = laid(late, "last_wg2", [P, S], F32, LAST_WG2_AT)
        w3_s = [laid(late, "w3_s%d" % a, [P, N], U8, W3_SCALES_AT[a]) for a in range(2)]
        z0_s = [laid(late, "z0_s%d" % half, [P, BANK], U8, Z0_SCALES_AT[half]) for half in range(2)]
        w4_s = laid(late, "w4_s", [P, N], U8, W4_SCALES_AT)
        w4_w = laid(late, "w4_w", [P, 2, N], U32, W4_WORDS_AT)
        first_h_b = laid(late, "first_h_b", [P, S], F32, FIRST_H_B_AT)
        v_s = [laid(tables, "v_s%d" % a, [P, S], U8, V_SCALES_AT[a]) for a in range(2)]
        second_h_b = laid(tables, "second_h_b", [P, S], F32, SECOND_H_B_AT)
        own_h_b = {0: first_h_b, 1: second_h_b}
        w3_w = [held("w3_w%d" % a, [P, N], U32) for a in range(2)]
        wg1_t = held("wg1_t", [P, S], F32)
        wg2_t = held("wg2_t", [P, S], F32)
        wg2_neg = held("wg2_neg", [P, S], F32)
        gain_dealt = held("gain_dealt", [P, PACK], F32)
        gain_rows = held("gain_rows", [P, SLICES - TURNED], F32)
        ident = held("ident", [P, P], F32)
        pages_a = [laid(tables, "page_a%d" % i, [P, T2], F32, at) for i, at in enumerate(PAGE_A_AT)]
        pages_b = [held("page_b%d" % i, [P, T2], F32) for i in range(2)]
        w2_w = [held("w2_w%d" % i, [P, P * n], U32) for i, (s0, n) in enumerate(W2_PIECES)]
        w2_s = [held("w2_s%d" % i, [P, P * n], U8) for i, (s0, n) in enumerate(W2_PIECES)]
        z0_w = [held("z0_w%d" % half, [P, BANK], U32) for half in range(2)]
        z1_w = [held("z1_w%d" % pair, [P, PAIR], U32) for pair in range(T2 // PAIR)]
        z1_s = [held("z1_s%d" % pair, [P, PAIR], U8) for pair in range(T2 // PAIR)]
        y_w = [held("y_w%d" % c, [P, width], U32) for c, (m0, width) in enumerate(CHUNKS)]
        y_s = held("y_s", [P, T2], U8)
        excess = [laid(late, "excess%d" % half, [P, 4, PACK, P], F32, EXCESS_AT[half]) for half in range(2)]
        placed = [held("placed%d" % half, [P, 4, PACK, P], F32) for half in range(2)]
        z1_turned = [held("z1_turned%d" % pair, [P, 2, 2, P, 2], BF16) for pair in range(T2 // PAIR)]

        for scale_tile in (tab_s, w1_s):
            zero_bytes(nc.vector, scale_tile)
        nc.vector.memset(pages_b[0][:], 0.0)
        make_identity(nc, ident[:])
        nc.gpsimd.memset(pages_b[1][:], 0.0)

        z1_acc, w4_raw, peak, weight_b, y_acc = {}, {}, {}, {}, {}
        w2_raw, w3_raw, w2_stage, w3_stage, f_rows = {}, {}, {}, {}, {}
        h_a, h_b, z0_rows, z0_woven, z1_woven, y_rows, y_woven = {}, {}, {}, {}, {}, {}, {}

        def page_a(s):
            return pages_a[s % len(pages_a)]

        def page_b(s):
            return pages_b[s % len(pages_b)]

        def row_gain(s):
            return gain_rows[:, s - TURNED : s - TURNED + 1]

        def load_w2(i):
            s0, n = W2_PIECES[i]
            w2_raw[i] = raw_tile([P, PACK, P * n], F32)
            nc.sync.dma_start(out=w2_raw[i][:], in_=w2[:, P * s0 : P * (s0 + n)].rearrange("(p j) c -> p j c", j=PACK))

        def cast_w2(i):
            n = W2_PIECES[i][1]
            w2_stage[i] = stage_tile([P, P * n * PACK])
            nc.scalar.copy(
                out=w2_stage[i][:].rearrange("p (c i j) -> p c j i", i=RUN, j=PACK),
                in_=w2_raw[i][:].rearrange("p j (c i) -> p c j i", i=RUN),
            )

        def quantize_w2(i):
            nc.vector.quantize_mx(out=w2_w[i][:].bitcast(FP8X4), scales=w2_s[i][:], in_=w2_stage[i][:])

        def load_w3(a):
            w3_raw[a] = raw_tile([P, PACK, N], F32)
            nc.sync.dma_start(out=w3_raw[a][:], in_=w3[KP * a : KP * (a + 1), :].rearrange("(p j) c -> p j c", j=PACK))

        def cast_w3(a, half):
            if half == 0:
                w3_stage[a] = stage_tile([P, PACK, P, PACK])
            quads, cols = P // 2, N // 2
            nc.scalar.copy(
                out=w3_stage[a][:, :, quads * half : quads * (half + 1), :].rearrange("p t q j -> p q j t"),
                in_=w3_raw[a][:, :, cols * half : cols * (half + 1)].rearrange("p j (q t) -> p q j t", t=PACK),
            )

        def quantize_w3(a):
            nc.vector.quantize_mx(
                out=w3_w[a][:].bitcast(FP8X4), scales=w3_s[a][:], in_=w3_stage[a][:].rearrange("p t q j -> p (t q j)")
            )

        def load_w4():
            w4_raw["words"] = raw_tile([P, 2, N], U32)
            nc.sync.dma_start(
                out=w4_raw["words"][:].bitcast(I32), in_=w4_words.rearrange("a p c i -> p a (c i)").bitcast(I32)
            )
            zero_bytes(nc.gpsimd, w4_raw_s)
            for q in range(QUADS):
                nc.sync.dma_start(
                    out=w4_raw_s[32 * q : 32 * q + 8, :].bitcast(I32),
                    in_=w4_scales[:, 4 * q : 4 * q + 4, :].bitcast(I32),
                )

        def deal_w4():
            nc.vector.tensor_copy(
                out=w4_w[:].bitcast(I32).rearrange("p a (t c i) -> p a c t i", t=PACK, i=RUN),
                in_=w4_raw["words"][:].bitcast(I32).rearrange("p a (c i t) -> p a c t i", t=PACK, i=RUN),
            )
            nc.vector.tensor_copy(
                out=w4_s[:].rearrange("p (t q) -> p q t", t=PACK),
                in_=w4_raw_s[:].rearrange("p (q t) -> p q t", t=PACK),
            )

        def load_forecast(s):
            place = s % len(ROWS_AT)
            f_rows[s] = laid(tables, "rows%d" % place, [P, T2], F32, ROWS_AT[place])
            nc.sync.dma_start(out=f_rows[s][:], in_=forecast[P * s : P * (s + 1), :])

        def features_a(s):
            acc = bank("first", [P, S])
            for a in range(2):
                nc.tensor.matmul_mx(
                    out=acc[:],
                    lhsT=w1_w[:, a, 2 * P * s : 2 * P * (s + 1)].bitcast(FP4X4),
                    lhsT_scale=w1_s[:, H * a + P * s : H * a + P * (s + 1)],
                    rhs=v_w[a][:].bitcast(FP8X4),
                    rhs_scale=v_s[a][:],
                    start=(a == 0),
                    stop=(a == 1),
                )
            h_a[s] = feature_tile()
            nc.scalar.activation(out=h_a[s][:], in_=acc[:], func=ACT.Tanh, scale=(-1.0 if s < TURNED else 1.0))

        def features_b(s):
            i = max(j for j, (s0, n) in enumerate(W2_PIECES) if s0 <= s)
            cols = slice(P * (s - W2_PIECES[i][0]), P * (s - W2_PIECES[i][0] + 1))
            acc = bank("first", [P, S])
            nc.tensor.matmul_mx(
                out=acc[:],
                lhsT=w2_w[i][:, cols].bitcast(FP8X4),
                lhsT_scale=w2_s[i][:, cols],
                rhs=v2_w[:].bitcast(FP8X4),
                rhs_scale=v2_s[:],
                start=True,
                stop=True,
            )
            h_b[s] = own_h_b[s] if s in own_h_b else feature_tile()
            nc.scalar.activation(out=h_b[s][:], in_=acc[:], func=ACT.Silu)

        def weigh_b(s):
            weight_b[s] = wg2_neg
            if s >= TURNED:
                weight_b[s] = last_wg2 if s == LAST else held("wg2_gain%d" % s, [P, S], F32)
                nc.scalar.activation(out=weight_b[s][:], in_=wg2_t[:], func=ACT.Copy, scale=row_gain(s))

        def place_a(s):
            nc.vector.tensor_tensor(page_a(s)[:].indirect(idx3[:]), h_a[s][:], wg1_t[:], ALU.mult)

        def place_b(s):
            nc.vector.tensor_tensor(page_b(s)[:].indirect(idx4[:]), h_b[s][:], weight_b[s][:], ALU.mult)

        def add_turned(out, first, second):
            nc.tensor.matmul(out, lhsT=first, rhs=ident[:], start=True, stop=False, is_transpose=True)
            nc.tensor.matmul(out, lhsT=second, rhs=ident[:], start=False, stop=True, is_transpose=True)

        def block_of(tile, b):
            return tile[:, P * b : P * (b + 1)]

        def turned_half(half, first, second):
            acc = bank("turned", [P, 4, P])
            for b in range(4):
                add_turned(acc[:, b, :], block_of(first, 4 * half + b), block_of(second, 4 * half + b))
            return acc

        def turn_sum(s, first, second, dest, func, scale):
            for half in range(2):
                acc = turned_half(half, first, second)
                nc.scalar.activation(
                    out=dest[half][:, :, :, 32 * s : 32 * (s + 1)],
                    in_=acc[:].rearrange("m b (p t) -> m b t p", t=PACK),
                    func=func,
                    scale=scale,
                )

        def turn_excess(s):
            turn_sum(s, f_rows[s], page_a(s), excess, ACT.Relu, 1.0)

        def turn_placed(s):
            turn_sum(s, page_a(s), page_b(s), placed, ACT.Copy, -1.0)

        def z0_back(half):
            z0_rows[half] = stage_tile([P, PACK, BANK])
            for t in range(PACK):
                acc = bank("back", [P, 4, P])
                for b in range(4):
                    add_turned(acc[:, b, :], excess[half][:, b, t, :], placed[half][:, b, t, :])
                nc.scalar.activation(
                    out=z0_rows[half][:, t, :],
                    in_=acc[:].rearrange("p b m -> p (b m)"),
                    func=ACT.Copy,
                    scale=gain_dealt[:, t : t + 1],
                )

        def z0_weave(half, part):
            z0_woven[half, part] = laid(
                late, "z0_woven%d%d" % (half, part), [P, PAIR * PACK], BF16, Z0_WOVEN_AT[half][part]
            )
            nc.scalar.copy(
                out=z0_woven[half, part][:].rearrange("p (c i t) -> p c t i", i=RUN, t=PACK),
                in_=z0_rows[half][:, :, PAIR * part : PAIR * (part + 1)].rearrange("p t (c i) -> p c t i", i=RUN),
            )

        def quantize_z0(half):
            for part in range(2):
                cols = slice(PAIR * part, PAIR * (part + 1))
                nc.vector.quantize_mx(
                    out=z0_w[half][:, cols].bitcast(FP8X4), scales=z0_s[half][:, cols], in_=z0_woven[half, part][:]
                )

        def make_peak(s):
            larger = laid(late, "larger%d" % s, [P, T2], F32, MAX_AT[s - TURNED])
            nc.vector.tensor_tensor(larger[:], page_a(s)[:], f_rows[s][:], ALU.max)
            peak[s] = laid(late, "peak%d" % s, [P, T2], F32, PEAK_AT[s - TURNED])
            nc.scalar.activation(out=peak[s][:], in_=larger[:], func=ACT.Copy, scale=row_gain(s))

        def round_z1(s, pair, acc):
            quarter = s - TURNED
            nc.scalar.copy(
                out=z1_turned[pair][:, :, :, 32 * quarter : 32 * (quarter + 1), :],
                in_=acc.rearrange("m b (p u e) -> m b u p e", u=2, e=2),
            )

        def turn_z1(s):
            for half in range(2):
                acc = turned_half(half, peak[s], page_b(s))
                for j in range(2):
                    round_z1(s, 2 * half + j, acc[:, 2 * j : 2 * j + 2, :])

        def turn_last(g, source, opens):
            b0, n = LAST_BANKS[g]
            for j in range(n):
                nc.tensor.matmul(
                    z1_acc[g][:, j, :],
                    lhsT=block_of(source, b0 + j),
                    rhs=ident[:],
                    start=(opens and j == 0),
                    stop=(not opens and j == n - 1),
                    is_transpose=True,
                )

        def weave_z1(pair):
            z1_woven[pair] = stage_tile([P, PAIR * PACK])
            acc = bank("turned", [P, 2, 2, P])
            for b in range(2):
                for u in range(2):
                    words = z1_turned[pair][:, b, u, :, :].rearrange("m p e -> m (p e)").bitcast(F32)
                    nc.tensor.transpose(acc[:, b, u, :], words, ident[:])
            nc.scalar.copy(
                out=z1_woven[pair][:].bitcast(F32).rearrange("p (b m u) -> p b m u", b=2, u=2),
                in_=acc[:].rearrange("p b u m -> p b m u"),
            )

        def quantize_z1(pair):
            nc.vector.quantize_mx(out=z1_w[pair][:].bitcast(FP8X4), scales=z1_s[pair][:], in_=z1_woven[pair][:])

        def second_pass(c, g, a):
            m0, width = CHUNKS[c]
            share = BANK // width
            t0 = share * (g // 2)
            if a == 0:
                y_acc[c, g] = bank(Y_BANKS[c][g], [P, share, width])
                half, first = divmod(m0, BANK)
                words, scales = z0_w[half], z0_s[half]
            else:
                pair, first = divmod(m0, PAIR)
                words, scales = z1_w[pair], z1_s[pair]
            cols = slice(first, first + width)
            for j in range(share):
                dealt = slice(P * (t0 + j), P * (t0 + j + 1))
                nc.tensor.matmul_mx(
                    out=y_acc[c, g][:, j, :],
                    lhsT=(w4_w[:, a, dealt] if g % 2 else w3_w[a][:, dealt]).bitcast(FP8X4),
                    lhsT_scale=w4_s[4 * a : P, dealt] if g % 2 else w3_s[a][:, dealt],
                    rhs=words[:, cols].bitcast(FP8X4),
                    rhs_scale=scales[:, cols],
                    start=(a == 0 and j == 0),
                    stop=(a == 1 and j == share - 1),
                )

        def finish_sum(c, g):
            if (c, g) not in EARLY:
                second_pass(c, g, 0)
            second_pass(c, g, 1)

        out_rows = out_0.rearrange("(p t) m -> p t m", t=PACK)
        out_words = out_1[0].rearrange("p m t -> p (m t)").bitcast(I32)

        def make_y(c):
            m0, width = CHUNKS[c]
            share = BANK // width
            y_rows[c] = laid(tables, "y_rows%d" % c, [P, PACK, width], F32, Y_ROWS_AT[c])
            for g in range(0, len(Y_BANKS[c]), 2):
                t0 = share * (g // 2)
                finish_sum(c, g)
                bent = feature_tile()
                nc.scalar.activation(out=bent[:], in_=y_acc[c, g][:].rearrange("p j m -> p (j m)"), func=ACT.Tanh)
                finish_sum(c, g + 1)
                rows = y_rows[c][:, t0 : t0 + share, :]
                nc.vector.tensor_tensor(
                    rows.rearrange("p j m -> p (j m)"), y_acc[c, g + 1][:].rearrange("p j m -> p (j m)"), bent[:], ALU.add
                )
                nc.sync.dma_start(out=out_rows[:, t0 : t0 + share, m0 : m0 + width], in_=rows)

        def weave_y(c):
            width = CHUNKS[c][1]
            y_woven[c] = stage_tile([P, width * PACK])
            woven = y_woven[c][:].rearrange("p (c i t) -> p c t i", i=RUN, t=PACK)
            rows = y_rows[c][:].rearrange("p t (c i) -> p c t i", i=RUN)
            if c < SCALAR_WEAVES:
                runs = P // RUN
                for first in range(0, width // RUN, runs):
                    nc.scalar.copy(out=woven[:, first : first + runs], in_=rows[:, first : first + runs])
            else:
                nc.vector.tensor_copy(out=woven, in_=rows)

        def quantize_y(c):
            m0, width = CHUNKS[c]
            cols = slice(m0, m0 + width)
            nc.vector.quantize_mx(out=y_w[c][:].bitcast(FP8X4), scales=y_s[:, cols], in_=y_woven[c][:])
            nc.sync.dma_start(out=out_words[:, cols], in_=y_w[c][:].bitcast(I32))

        nc.sync.dma_start(idx2[:], offs2)
        load_words(tab2_w, tab2_words[0])
        for q in range(QUADS):
            nc.sync.dma_start(
                out=tab2_s[32 * q : 32 * (q + 1), :].bitcast(I32),
                in_=tab2_scales[0, 4 * q : 4 * q + 4, :].bitcast(I32).unsqueeze(0).to_broadcast([8, 4, T3 // 4]),
            )
        load_w2(0)
        load_words(tab_w[0], tab_words[0])
        nc.sync.dma_start(idx[:], offs)
        nc.sync.dma_start(out=wg2_t[:], in_=wg2)
        nc.sync.dma_start(idx4[:], offs4)
        load_w2(1)
        with nc.allow_non_contiguous_dma(reason="one gain for each partition and slice"):
            nc.sync.dma_start(out=gain_rows[:], in_=gain[KP:H].rearrange("(s p) -> p s", p=P))
        load_scales(tab_s, tab_scales)
        load_words(tab_w[1], tab_words[1])
        nc.sync.dma_start(out=w1_w[:].bitcast(I32), in_=w1_words.rearrange("a p c -> p a c").bitcast(I32))
        load_scales(w1_s, w1_scales)
        load_w2(2)
        nc.sync.dma_start(out=wg1_t[:], in_=wg1)
        nc.sync.dma_start(idx3[:], offs3)

        cast_w2(0)
        nc.vector.tensor_copy(v2_w[:], tab2_w[:].indirect(idx2[:]))
        nc.vector.tensor_copy(v2_s[:], tab2_s[:].indirect(idx2[:]))
        quantize_w2(0)
        features_b(0)
        load_w3(0)
        load_forecast(0)
        nc.vector.tensor_copy(v_w[0][:], tab_w[0][:].indirect(idx[:]))
        nc.vector.tensor_scalar_mul(wg2_neg[:], wg2_t[:], -1.0)
        cast_w2(1)
        for s in range(LAST):
            weigh_b(s)
        nc.gpsimd.memset(pages_a[0][:], 0.0)
        place_b(0)
        quantize_w2(1)
        nc.vector.tensor_copy(v_w[1][:], tab_w[1][:].indirect(idx[:]))
        for a in range(2):
            nc.vector.tensor_copy(v_s[a][:], tab_s[:, T * a : T * (a + 1)].indirect(idx[:]))
        features_b(1)
        for page in pages_a[1:]:
            nc.gpsimd.memset(page[:], 0.0)
        load_forecast(1)
        load_w3(1)
        load_forecast(2)
        nc.sync.dma_start(out=gain_dealt[:], in_=gain[0:KP].rearrange("(p t) -> p t", t=PACK))

        features_a(0)
        place_b(1)
        features_a(1)
        cast_w2(2)
        cast_w3(0, 0)
        cast_w3(0, 1)
        place_a(0)
        features_a(2)
        features_b(2)
        turn_placed(0)
        turn_excess(0)
        load_forecast(3)
        place_a(1)
        quantize_w2(2)
        features_a(3)
        features_b(3)
        load_w4()
        turn_excess(1)
        load_forecast(4)

        for s in range(2, SLICES):
            place_a(s)
            ahead = {LAST - 2: None, LAST - 1: LAST, LAST: None}.get(s, s + 2)
            if ahead is not None:
                features_a(ahead)
                features_b(ahead)
            if s - 1 < TURNED:
                turn_placed(s - 1)
            else:
                turn_z1(s - 1)
            if s == 2:
                cast_w3(1, 0)
            if s in (TURNED, TURNED + 1):
                z0_back(s - TURNED)
            if s == LAST - 1:
                z0_weave(0, 0)
                z0_weave(0, 1)
            if s == LAST:
                z0_weave(1, 0)
                quantize_z0(0)
                quantize_w3(0)
                weigh_b(s)
                for c, g in EARLY:
                    second_pass(c, g, 0)
                make_peak(s)
                z0_weave(1, 1)
            place_b(s)
            if s < TURNED:
                turn_excess(s)
            elif s < LAST:
                make_peak(s)
            if s + len(ROWS_AT) < SLICES:
                load_forecast(s + len(ROWS_AT))
            if s == 2:
                cast_w3(1, 1)

        for g, (b0, n) in enumerate(LAST_BANKS):
            z1_acc[g] = bank("turned", [P, n, P])
            turn_last(g, peak[LAST], True)
        for g, (b0, n) in enumerate(LAST_BANKS):
            turn_last(g, page_b(LAST), False)
            for j in range(0, n, 2):
                round_z1(LAST, (b0 + j) // 2, z1_acc[g][:, j : j + 2, :])

        quantize_w3(1)
        deal_w4()
        quantize_z0(1)
        for pair in range(T2 // PAIR):
            weave_z1(pair)
            quantize_z1(pair)
        for c in range(len(CHUNKS)):
            make_y(c)
            if c > 0:
                quantize_y(c - 1)
            weave_y(c)
        quantize_y(len(CHUNKS) - 1)
        for q in range(QUADS):
            nc.sync.dma_start(
                out=out_2[0, 4 * q : 4 * q + 4, :].bitcast(I32), in_=y_s[32 * q : 32 * q + 4, :].bitcast(I32)
            )
